import numpy as np, ml_dtypes
CORES = [10,34,74,98]
N = 4
import mx_ref
BF = ml_dtypes.bfloat16
def f(rng, *shape):
    return mx_ref.flush((rng.standard_normal(shape, dtype=np.float32) * np.exp2(rng.integers(-2, 3, shape[:-1] + (1,)))).astype(BF))
def wide(rng, *shape, cols=0):
    v = rng.standard_normal(shape, dtype=np.float32) * np.exp2(rng.integers(-12, 13, shape)).astype(np.float32)
    if cols: v *= np.repeat(np.exp2(rng.integers(-cols, cols + 1, shape[:-2] + (1, shape[-1] // 4))) * (rng.random(shape[:-2] + (1, shape[-1] // 4)) > 0.0625), 4, axis=-1).astype(np.float32)
    return mx_ref.flush(v.astype(BF))
R, XC = 2048, 512
def lists(rng):
    return rng.integers(0, R, (N, N, 512))
def picks(L):
    return np.ascontiguousarray(L.reshape(N, N, 128, 4).transpose(0, 2, 1, 3)).reshape(N, 128, 4 * N).astype(np.int32)
def setup_inputs(rng):
    return {"x": f(rng, N, R, XC), "w": f(rng, N, R, 128), "pick": picks(lists(rng))}
def setup_inputs_alike(rng):
    d = setup_inputs(rng); L = lists(rng)
    L[:] = L[0, 0].copy()
    d["pick"] = picks(L); return d
def setup_inputs_giant(rng):
    d = setup_inputs(rng); L = lists(rng); big = {}
    for n in ("x", "w"):
        big[n] = 32 * np.arange(R // 32) + rng.integers(0, 32, (N, R // 32))
        m = np.ones((N, R, 1), np.float32)
        for r in range(N): m[r, big[n][r]] = 4096
        d[n] = (d[n].astype(np.float32) * m).astype(BF)
    for r in range(N):
        for s in range(N):
            for g in range(16):
                a, b = 32 * g + rng.permutation(32)[:2]
                L[r, s, a] = rng.choice(big["x"][s]); L[r, s, b] = rng.choice(big["w"][r])
    d["pick"] = picks(L); return d
def setup_inputs_repeat(rng):
    d = setup_inputs(rng); L = lists(rng)
    for r in range(N): L[r, (r + rng.integers(1, N)) % N] = rng.integers(0, R)
    d["pick"] = picks(L); return d
def setup_inputs_sorted(rng):
    d = setup_inputs(rng); L = lists(rng)
    L[:, :, 0] = 0; L[:, :, 1] = R - 1
    d["pick"] = picks(np.sort(L, axis=2)); return d
def setup_inputs_spread(rng):
    d = setup_inputs(rng); d["x"] = wide(rng, N, R, XC); d["w"] = wide(rng, N, R, 128); return d
def check_inputs(d):
    b = []
    for n in ("x", "w"):
        a = np.abs(np.asarray(d[n]).astype(np.float32))
        if not np.isfinite(a).all() or ((a != 0) & ((a < 2.0 ** -30) | (a > 2.0 ** 30))).any(): b.append(n)
    if d["pick"].min() < 0 or d["pick"].max() >= R: b.append("pick")
    return b
def rowtile(v, k):
    return np.ascontiguousarray(v[k].transpose(0, 2, 1)).reshape(128, -1)
def reference(x, w, pick):
    y = np.zeros((N, 128, N * XC), np.float32)
    for r in range(N):
        for s in range(N):
            k = pick[r][:, 4 * s:4 * s + 4]
            y[r][:, XC * s:XC * s + XC] = mx_ref.matmul(mx_ref.quantize(rowtile(w[r], k)), mx_ref.quantize(rowtile(x[s], k)))
    return {"y": y}

@@ -1,0 +1,352 @@
+from concourse.bass import DstId, RemoteDMATransfer, IndirectOffsetOnAxis
+from concourse.mybir import dt, AluOpType, ActivationFunctionType
+
+NR = 4
+XC = 512
+WC = 128
+ROWS = 2048
+WIN = 3
+
+SCRATCH = {
+    "pk": ("sbuf", [128, 16], "int32"),
+    "plo": ("sbuf", [128, 16], "int32"),
+    "phi": ("sbuf", [128, 16], "int32"),
+    "pls": ("sbuf", [128, 16], "int32"),
+    "pf": ("sbuf", [128, 128], "float32"),
+    "offs": ("sbuf", [128, 128], "uint16"),
+    "lu": ("sbuf", [128, 4], "int32"),
+    "lb": ("sbuf", [128, 4], "int32"),
+    "lc": ("sbuf", [128, 4], "int32"),
+    "lv": ("sbuf", [128, 4], "int32"),
+    "lw": ("sbuf", [128, 4], "int32"),
+    "lp": ("sbuf", [128, 4], "int32"),
+    "pf3": ("sbuf", [128, 128], "float32"),
+    "offs3": ("sbuf", [128, 128], "uint16"),
+    "ones": ("sbuf", [128, 128], "float32"),
+    "ident": ("sbuf", [128, 128], "float32"),
+    "wb": ("sbuf", [128, 2048], "bfloat16"),
+    "wf": ("sbuf", [128, 2048], "float32"),
+    "wtr": ("sbuf", [128, 2048], "bfloat16"),
+    "wg": ("sbuf", [128, 2048], "float32"),
+    "xb": ("sbuf", [128, 8192], "bfloat16"),
+    "xv": ("sbuf", [128, 8192], "bfloat16"),
+    "xg": ("sbuf", [128, 2048], "float32"),
+    "x3": ("sbuf", [128, 4, 512], "bfloat16"),
+    "ys": ("sbuf", [128, 2048], "float32"),
+    "ps_p": ("psum", [128, 512], "float32"),
+    "ps_w": ("psum", [128, 1024], "float32"),
+    "ps_x": ("psum", [128, 1024], "float32"),
+    "ps_y": ("psum", [128, 1536], "float32"),
+}
+for _k in range(NR):
+    if _k != WIN:
+        SCRATCH["xs%d" % _k] = ("sbuf", [128, 2048], "bfloat16")
+        SCRATCH["xt%d" % _k] = ("sbuf", [128, 2048], "bfloat16")
+    SCRATCH["xq%d" % _k] = ("sbuf", [128, XC], "float8_e4m3fn_x4")
+    SCRATCH["xp%d" % _k] = ("sbuf", [128, XC], "uint8")
+    SCRATCH["wt%d" % _k] = ("sbuf", [128, 512], "bfloat16")
+    SCRATCH["wq%d" % _k] = ("sbuf", [128, WC], "float8_e4m3fn_x4")
+    SCRATCH["wp%d" % _k] = ("sbuf", [128, WC], "uint8")
+    if _k:
+        SCRATCH["li%d" % _k] = ("sbuf", [128, 4], "int32")
+        SCRATCH["rq%d" % _k] = ("sbuf", [128, XC], "float8_e4m3fn_x4")
+        SCRATCH["rp%d" % _k] = ("sbuf", [128, XC], "uint8")
+
+SEMAPHORES = ["id0", "id1", "pk", "wl", "pa", "pb", "pc", "pf", "pt", "off", "wc0", "wc1", "gs",
+              "ls1", "lsent", "csent", "la", "lv", "lw", "lp", "lm", "ld1", "ld2", "ld3", "pt3", "off3",
+              "xz", "hv", "hs",
+              "mm1", "mm2", "mm0", "mm3a", "mm3b", "ev1", "ev2", "ev0", "ev3a", "ev3b",
+              "st1", "st2", "st0", "st3a", "st3b"]
+SEMAPHORES += ["%s%d" % (n, k) for n in ("wi", "we", "wv", "wd", "qw", "xc", "qx", "xl", "xf", "xe") for k in range(NR)]
+SEMAPHORES += ["%s%d" % (n, k) for n in ("lst", "arr") for k in range(1, NR)]
+SEMAPHORES += ["ga%d%d" % (k, t) for k in range(NR) if k != WIN for t in range(4)]
+
+COPY = ActivationFunctionType.Copy
+AND, SHR, ADD, MULT = AluOpType.bitwise_and, AluOpType.arith_shift_right, AluOpType.add, AluOpType.mult
+
+
+def rank_program(g, core, T, topo):
+    me = T.rank_of(core)
+    if me is None:
+        return
+    S = T.sem
+    cores = T.cores
+    v, a, te, sy = g.vector, g.scalar, g.tensor, g.sync
+
+    def direct(k):
+        return sum(1 for r in range(NR)
+                   if topo.same_plane(topo.chip(cores[r]), topo.chip(cores[(r + k) % NR])))
+    steps = [0] + sorted(range(1, NR), key=direct)
+    to = [(me + steps[k]) % NR for k in range(NR)]
+    frm = [(me - steps[k]) % NR for k in range(NR)]
+    worder = [1, 0, 2, 3]
+
+    def dst(r):
+        rid, pid, _ = topo.addr(cores[r])
+        return rid, pid
+
+    def bits(engs):
+        return sum(1 << e for e in engs)
+
+    off_chip = topo.engines(core, cores[frm[1]])
+    la, lb, lc = off_chip[0:4], off_chip[4:6], off_chip[6:8]
+
+    sy.dma_start(T.pk[:], T.pick[:]).then_inc(S.pk, 16)
+    sy.dma_start(T.wb[:], T.w[:]).then_inc(S.wl, 16)
+    for n in range(16):
+        z, q = n // 4, n % 4
+        if n == 2:
+            sy.wait_ge(S.ls1, len(la))
+        if q == 0 and z >= 2:
+            sy.wait_ge(S["xl%d" % (z - 2)], 64)
+        sy.dma_start(T.xb[32 * q:32 * q + 32, 2048 * z:2048 * z + 2048],
+                     T.x[512 * z:512 * z + 512, 128 * q:128 * q + 128]).then_inc(S["xl%d" % z], 16)
+
+    v.memset(T.ones[:], 1.0).then_inc(S.id0, 1)
+    v.wait_ge(S.pk, 16)
+    v.tensor_scalar(T.plo[:], T.pk[:], 15, None, AND).then_inc(S.pa, 1)
+    v.tensor_scalar(T.phi[:], T.pk[:], 4, None, SHR).then_inc(S.pb, 1)
+    v.wait_ge(S.pa, 1)
+    v.tensor_scalar(T.pls[:], T.plo[:], 128, None, MULT).then_inc(S.pc, 1)
+    v.wait_ge(S.pb, 1)
+    v.wait_ge(S.pc, 1)
+    for q in range(8):
+        v.tensor_tensor(T.pf[:, 16 * q:16 * q + 16], T.pls[:], T.phi[:], ADD).then_inc(S.pf, 1)
+    v.wait_ge(S.wl, 16)
+    for h in range(2):
+        v.tensor_copy(T.wf[:, 1024 * h:1024 * h + 1024], T.wb[:, 1024 * h:1024 * h + 1024]).then_inc(S["wc%d" % h], 1)
+    v.wait_ge(S.pt, 1)
+    v.tensor_copy(T.offs[:], T.ps_p[:, 0:128]).then_inc(S.off, 1)
+    li = T["li%d" % WIN]
+    v.wait_ge(S["lst%d" % WIN], len(lc))
+    v.tensor_scalar(T.lu[:], li[:], 5, 48, SHR, AND).then_inc(S.la, 1)
+    v.tensor_scalar(T.lb[:], li[:], 15, None, AND).then_inc(S.la, 1)
+    v.tensor_scalar(T.lc[:], li[:], 4, 31, SHR, AND).then_inc(S.la, 1)
+    v.wait_ge(S.la, 3)
+    v.tensor_tensor(T.lv[:], T.lu[:], T.lb[:], ADD).then_inc(S.lv, 1)
+    v.wait_ge(S.lv, 1)
+    v.tensor_scalar(T.lw[:], T.lv[:], 128, None, MULT).then_inc(S.lw, 1)
+    v.wait_ge(S.lw, 1)
+    v.tensor_tensor(T.lp[:], T.lw[:], T.lc[:], ADD).then_inc(S.lp, 1)
+    v.wait_ge(S.lp, 1)
+    for m in range(4):
+        v.tensor_scalar(T.pf3[:, 4 * m:4 * m + 4], T.lp[:], 32 * m, None, ADD).then_inc(S.lm, 1)
+    v.wait_ge(S.lm, 4)
+    v.tensor_copy(T.pf3[:, 16:32], T.pf3[:, 0:16]).then_inc(S.ld1, 1)
+    v.wait_ge(S.ld1, 1)
+    v.tensor_copy(T.pf3[:, 32:64], T.pf3[:, 0:32]).then_inc(S.ld2, 1)
+    v.wait_ge(S.ld2, 1)
+    v.tensor_copy(T.pf3[:, 64:128], T.pf3[:, 0:64]).then_inc(S.ld3, 1)
+
+    for b in range(4):
+        a.wait_ge(S["wi%d" % b], 4)
+        o = 512 * (b % 2)
+        a.activation(T.wtr[:, 512 * b:512 * b + 512], T.ps_w[:, o:o + 512], COPY).then_inc(S["we%d" % b], 1)
+    a.wait_ge(S.off, 1)
+    for b in range(4):
+        a.wait_ge(S["we%d" % b], 1)
+    a.activation(T.wg[:], T.wtr[:].indirect(T.offs[:, 0:128]), COPY).then_inc(S.gs, 1)
+
+    te.wait_ge(S.id1, 1)
+    te.wait_ge(S.pf, 8)
+    te.transpose(T.ps_p[:, 0:128], T.pf[:], T.ident[:]).then_inc(S.pt, 1)
+    for b in range(4):
+        if b % 2 == 0:
+            te.wait_ge(S["wc%d" % (b // 2)], 1)
+        if b >= 2:
+            te.wait_ge(S["we%d" % (b - 2)], 1)
+        for i in range(4):
+            c = 4 * b + i
+            o = 512 * (b % 2) + 128 * i
+            te.transpose(T.ps_w[:, o:o + 128], T.wf[:, 128 * c:128 * c + 128], T.ident[:]).then_inc(S["wi%d" % b], 1)
+    te.wait_ge(S.off, 1)
+    te.wait_ge(S.ld3, 1)
+    te.transpose(T.ps_p[:, 128:256], T.pf3[:], T.ident[:]).then_inc(S.pt3, 1)
+
+    def wturn(n):
+        k, o = worder[n], 512 * (n % 2)
+        if n >= 2:
+            te.wait_ge(S["wd%d" % worder[n - 2]], 1)
+        for t in range(4):
+            te.transpose(T.ps_w[:, o + t:o + 512:4], T.wg[:, 4 * frm[k] + t:2048:16], T.ident[:]).then_inc(S["wv%d" % k], 1)
+
+    def wevac(n):
+        k, o = worder[n], 512 * (n % 2)
+        a.wait_ge(S["wv%d" % k], 4)
+        a.activation(T["wt%d" % k][:], T.ps_w[:, o:o + 512], COPY).then_inc(S["wd%d" % k], 1)
+
+    te.wait_ge(S.gs, 1)
+    wturn(0)
+    wturn(1)
+    te.wait_ge(S.hv, 1)
+    te.wait_ge(S.hs, 1)
+    for m in range(4):
+        if m >= 2:
+            te.wait_ge(S["xe%d" % (m - 2)], 1)
+        o = 512 * (m % 2)
+        for t in range(4):
+            te.transpose(T.ps_x[:, o + t:o + 512:4], T.xg[:, 4 * m + t:2048:16], T.ident[:]).then_inc(S["xf%d" % m], 1)
+    wturn(2)
+    wturn(3)
+
+    a.wait_ge(S.off3, 1)
+    a.wait_ge(S.xz, 4)
+    a.activation(T.xg[:, 1024:2048], T.xv[:].indirect(T.offs3[:, 64:128]), COPY).then_inc(S.hs, 1)
+    wevac(0)
+    wevac(1)
+    for m in range(4):
+        a.wait_ge(S["xf%d" % m], 4)
+        o = 512 * (m % 2)
+        a.activation(T.x3[:, :, 128 * m:128 * m + 128], T.ps_x[:, o:o + 512], COPY).then_inc(S["xe%d" % m], 1)
+    wevac(2)
+    wevac(3)
+
+    def xcopy(k, t):
+        v.wait_ge(S["ga%d%d" % (k, t)], 16)
+        v.tensor_copy(T["xt%d" % k][:, t:2048:4], T["xs%d" % k][:, 512 * t:512 * t + 512]).then_inc(S["xc%d" % k], 1)
+
+    def xquant(k):
+        v.wait_ge(S["xc%d" % k], 4)
+        v.quantize_mx(T["xq%d" % k][:], T["xp%d" % k][:], T["xt%d" % k][:]).then_inc(S["qx%d" % k], 1)
+
+    def wquant(n):
+        k = worder[n]
+        v.wait_ge(S["wd%d" % k], 1)
+        v.quantize_mx(T["wq%d" % k][:], T["wp%d" % k][:], T["wt%d" % k][:]).then_inc(S["qw%d" % k], 1)
+
+    def xturn(z):
+        v.wait_ge(S["xl%d" % z], 64)
+        v.transpose(T.xv[:, 2048 * z:2048 * z + 2048], T.xb[:, 2048 * z:2048 * z + 2048]).then_inc(S.xz, 1)
+
+    xturn(0)
+    v.wait_ge(S.pt3, 1)
+    v.tensor_copy(T.offs3[:], T.ps_p[:, 128:256]).then_inc(S.off3, 1)
+    xturn(1)
+    xcopy(1, 0)
+    xcopy(1, 1)
+    xcopy(1, 2)
+    xturn(2)
+    xcopy(1, 3)
+    xquant(1)
+    xturn(3)
+    v.wait_ge(S.off3, 1)
+    v.wait_ge(S.xz, 4)
+    v.tensor_copy(T.xg[:, 0:1024], T.xv[:].indirect(T.offs3[:, 0:64])).then_inc(S.hv, 1)
+    for t in range(4):
+        xcopy(2, t)
+    xquant(2)
+    for m in range(4):
+        v.wait_ge(S["xe%d" % m], 1)
+    for q in range(4):
+        v.quantize_mx(T["xq%d" % WIN][:, 128 * q:128 * q + 128], T["xp%d" % WIN][:, 128 * q:128 * q + 128],
+                      T.x3[:, q, :]).then_inc(S["qx%d" % WIN], 1)
+    wquant(0)
+    wquant(1)
+    for t in range(4):
+        xcopy(0, t)
+    xquant(0)
+    wquant(2)
+    wquant(3)
+
+    g.wait_ge(S.id0, 1)
+    g.affine_select(T.ident[:], T.ones[:], [[-1, 128]], AluOpType.is_equal, 0.0, 0, 1).then_inc(S.id1, 1)
+
+    def listmove(k, engs):
+        s = frm[k]
+        rid, pid = dst(s)
+        return RemoteDMATransfer(dst_ids=[DstId(rid=rid, pnc=pid)], dma_engine_mask=bits(engs),
+                                 remote_sem=S["lst%d" % k],
+                                 srcs=[T.pk[:, 4 * s:4 * s + 4]], dsts=[T["li%d" % k][:]])
+
+    def gather(k, t):
+        idx = T["li%d" % k][:, t:t + 1] if k else T.pk[:, 4 * me + t:4 * me + t + 1]
+        g.indirect_dma_start(T["xs%d" % k][:, 512 * t:512 * t + 512], None, T.x[:],
+                             IndirectOffsetOnAxis(ap=idx, axis=0), bounds_check=ROWS - 1).then_inc(S["ga%d%d" % (k, t)], 16)
+
+    def send_fused(k):
+        e = topo.engines(core, cores[to[k]])
+        rid, pid = dst(to[k])
+        parts = [e[0:2], e[2:4], e[4:6], e[6:7], e[7:8]]
+        tr = []
+        for i, p in enumerate(parts):
+            if i < 4:
+                src = T["xq%d" % k][:, 128 * i:128 * i + 128].bitcast(dt.uint8)
+                d = T["rq%d" % k][:, 128 * i:128 * i + 128].bitcast(dt.uint8)
+            else:
+                src, d = T["xp%d" % k][:], T["rp%d" % k][:]
+            tr.append(RemoteDMATransfer(dst_ids=[DstId(rid=rid, pnc=pid)], dma_engine_mask=bits(p),
+                                        remote_sem=S["arr%d" % k], srcs=[src], dsts=[d]))
+        g.remote_dma_fused(tr, local_sem=S.csent)
+        return sum(len(p) for p in parts)
+
+    def send_two(k):
+        e = topo.engines(core, cores[to[k]])
+        rid, pid = dst(to[k])
+        g.remote_dma(T["rq%d" % k][:].bitcast(dt.uint8), T["xq%d" % k][:].bitcast(dt.uint8),
+                     S["arr%d" % k], S.csent, pid, rid, bits(e))
+        g.remote_dma(T["rp%d" % k][:], T["xp%d" % k][:], S["arr%d" % k], S.csent, pid, rid, bits(e))
+        return 2 * len(e)
+
+    g.wait_ge(S.pk, 16)
+    g.remote_dma_fused([listmove(1, la)], local_sem=S.ls1)
+    gather(0, 0)
+    g.remote_dma_fused([listmove(2, lb), listmove(3, lc)], local_sem=S.lsent)
+    gather(0, 1)
+    g.wait_ge(S.lst1, len(la))
+    for t in range(4):
+        gather(1, t)
+    g.wait_ge(S.lst2, len(lb))
+    for t in range(3):
+        gather(2, t)
+    g.wait_ge(S.qx1, 1)
+    n1 = send_fused(1)
+    gather(2, 3)
+    gather(0, 2)
+    gather(0, 3)
+    g.wait_ge(S.qx2, 1)
+    n2 = send_two(2)
+    g.wait_ge(S["qx%d" % WIN], 4)
+    n3 = send_two(WIN)
+    g.wait_ge(S.lsent, len(lb) + len(lc))
+    g.wait_ge(S.csent, n1 + n2 + n3)
+
+    bank = {1: 0, 0: 512, 2: 1024}
+    narr = {1: n1, 2: n2}
+    for k in worder[:3]:
+        o = bank[k]
+        te.wait_ge(S["qw%d" % k], 1)
+        if k:
+            te.wait_ge(S["arr%d" % k], narr[k])
+            xq, xp = T["rq%d" % k], T["rp%d" % k]
+        else:
+            te.wait_ge(S.qx0, 1)
+            xq, xp = T.xq0, T.xp0
+        te.matmul_mx(T.ps_y[:, o:o + 512], T["wq%d" % k][:], T["wp%d" % k][:], xq[:], xp[:], True, True).then_inc(S["mm%d" % k], 1)
+    te.wait_ge(S.qw3, 1)
+    te.wait_ge(S.ev1, 1)
+    te.wait_ge(S.ev0, 1)
+    te.wait_ge(S.arr3, n3)
+    te.matmul_mx(T.ps_y[:, 0:256], T.wq3[:], T.wp3[:], T.rq3[:, 0:256], T.rp3[:, 0:256], True, True).then_inc(S.mm3a, 1)
+    te.matmul_mx(T.ps_y[:, 512:768], T.wq3[:], T.wp3[:], T.rq3[:, 256:512], T.rp3[:, 256:512], True, True).then_inc(S.mm3b, 1)
+
+    def ycols(k, lo=0, hi=XC):
+        b = XC * frm[k]
+        return slice(b + lo, b + hi)
+
+    for k in worder[:3]:
+        o = bank[k]
+        a.wait_ge(S["mm%d" % k], 1)
+        a.activation(T.ys[:, ycols(k)], T.ps_y[:, o:o + 512], COPY).then_inc(S["ev%d" % k], 1)
+        sy.wait_ge(S["ev%d" % k], 1)
+        sy.dma_start(T.y[:, ycols(k)], T.ys[:, ycols(k)]).then_inc(S["st%d" % k], 16)
+    v.wait_ge(S.mm3a, 1)
+    v.tensor_copy(T.ys[:, ycols(3, 0, 256)], T.ps_y[:, 0:256]).then_inc(S.ev3a, 1)
+    sy.wait_ge(S.ev3a, 1)
+    sy.dma_start(T.y[:, ycols(3, 0, 256)], T.ys[:, ycols(3, 0, 256)]).then_inc(S.st3a, 16)
+    a.wait_ge(S.mm3b, 1)
+    a.activation(T.ys[:, ycols(3, 256, 512)], T.ps_y[:, 512:768], COPY).then_inc(S.ev3b, 1)
+    a.wait_ge(S.ev3b, 1)
+    a.dma_start(T.y[:, ycols(3, 256, 512)], T.ys[:, ycols(3, 256, 512)]).then_inc(S.st3b, 16)
+    for n in ("st1", "st2", "st0", "st3a"):
+        sy.wait_ge(S[n], 16)
+    a.wait_ge(S.st3b, 16)

@@ -5,23 +5,38 @@ NR = 4
 XC = 512
 WC = 128
 ROWS = 2048
-WIN = 3
+WINS = (2, 3)
+DMAS = (1, 0)
+
+CFG = {
+    "depth": 6,
+    "cut": {2: 64, 3: 40},
+    "last": 3,
+    "v": ["pos", "woff", "turn0", "turn1", "pf", "turn2", "offs", "turn3", "g2", "back2", "g3", "back3", "q1", "q2", "wq1",
+          "c00", "c01", "qh0", "qh1", "wq2", "c02", "wq0", "wq3", "c03", "q0", "ya"],
+    "a": ["cv0", "cv1", "we0", "cv2", "we1", "cv3", "we2", "we3", "wg1", "wg2", "g2", "g3", "c10", "c11", "c12", "c13",
+          "wd1", "wg0", "wd2", "wg3", "wd0", "wd3", "y1", "y2", "y0", "yb"],
+    "t": ["wf0", "wf1", "wf2", "wf3", "offs", "wb1", "wb2", "wb0", "wb3", "mm1", "mm2", "mm0", "mm3"],
+    "g": ["l1", "l23", "ga00", "wl", "ga10", "ga11", "ga12", "ga13", "ga01", "ga02", "s1", "s2", "ga03", "sh0", "sh1"],
+    "s": ["ex2", "ex3", "st1", "st2", "st0", "sta"],
+}
 
 SCRATCH = {
     "pk": ("sbuf", [128, 16], "int32"),
-    "plo": ("sbuf", [128, 16], "int32"),
-    "phi": ("sbuf", [128, 16], "int32"),
-    "pls": ("sbuf", [128, 16], "int32"),
-    "pf": ("sbuf", [128, 128], "float32"),
-    "offs": ("sbuf", [128, 128], "uint16"),
-    "lu": ("sbuf", [128, 4], "int32"),
-    "lb": ("sbuf", [128, 4], "int32"),
-    "lc": ("sbuf", [128, 4], "int32"),
-    "lv": ("sbuf", [128, 4], "int32"),
-    "lw": ("sbuf", [128, 4], "int32"),
-    "lp": ("sbuf", [128, 4], "int32"),
-    "pf3": ("sbuf", [128, 128], "float32"),
-    "offs3": ("sbuf", [128, 128], "uint16"),
+    "pk2": ("sbuf", [128, 16], "int32"),
+    "lq": ("sbuf", [128, 4, 16], "int32"),
+    "lu": ("sbuf", [128, 16], "int32"),
+    "lb": ("sbuf", [128, 16], "int32"),
+    "lc": ("sbuf", [128, 16], "int32"),
+    "lv": ("sbuf", [128, 16], "int32"),
+    "lw": ("sbuf", [128, 16], "int32"),
+    "px": ("sbuf", [128, 16], "float32"),
+    "pw": ("sbuf", [128, 128], "float32"),
+    "pwt": ("sbuf", [128, 128], "float32"),
+    "offw": ("sbuf", [128, 128], "uint16"),
+    "lanes": ("sbuf", [128, 32], "float32"),
+    "pf": ("sbuf", [128, 256], "float32"),
+    "offx": ("sbuf", [128, 256], "uint16"),
     "ones": ("sbuf", [128, 128], "float32"),
     "ident": ("sbuf", [128, 128], "float32"),
     "wb": ("sbuf", [128, 2048], "bfloat16"),
@@ -30,36 +45,38 @@ SCRATCH = {
     "wg": ("sbuf", [128, 2048], "float32"),
     "xb": ("sbuf", [128, 8192], "bfloat16"),
     "xv": ("sbuf", [128, 8192], "bfloat16"),
-    "xg": ("sbuf", [128, 2048], "float32"),
-    "x3": ("sbuf", [128, 4, 512], "bfloat16"),
     "ys": ("sbuf", [128, 2048], "float32"),
     "ps_p": ("psum", [128, 512], "float32"),
-    "ps_w": ("psum", [128, 1024], "float32"),
-    "ps_x": ("psum", [128, 1024], "float32"),
-    "ps_y": ("psum", [128, 1536], "float32"),
+    "ps_w": ("psum", [128, 1536], "float32"),
+    "ps_y": ("psum", [128, 2048], "float32"),
 }
 for _k in range(NR):
-    if _k != WIN:
+    if _k in WINS:
+        SCRATCH["xg%d" % _k] = ("sbuf", [128, 2048], "bfloat16")
+        SCRATCH["ex%d" % _k] = ("sbuf", [128, 4, 512], "bfloat16")
+        SCRATCH["li%d" % _k] = ("sbuf", [128, 4], "float32")
+    else:
         SCRATCH["xs%d" % _k] = ("sbuf", [128, 2048], "bfloat16")
-        SCRATCH["xt%d" % _k] = ("sbuf", [128, 2048], "bfloat16")
+        if _k:
+            SCRATCH["li%d" % _k] = ("sbuf", [128, 4], "int32")
+    SCRATCH["xt%d" % _k] = ("sbuf", [128, 2048], "bfloat16")
     SCRATCH["xq%d" % _k] = ("sbuf", [128, XC], "float8_e4m3fn_x4")
     SCRATCH["xp%d" % _k] = ("sbuf", [128, XC], "uint8")
     SCRATCH["wt%d" % _k] = ("sbuf", [128, 512], "bfloat16")
     SCRATCH["wq%d" % _k] = ("sbuf", [128, WC], "float8_e4m3fn_x4")
     SCRATCH["wp%d" % _k] = ("sbuf", [128, WC], "uint8")
     if _k:
-        SCRATCH["li%d" % _k] = ("sbuf", [128, 4], "int32")
         SCRATCH["rq%d" % _k] = ("sbuf", [128, XC], "float8_e4m3fn_x4")
         SCRATCH["rp%d" % _k] = ("sbuf", [128, XC], "uint8")
 
-SEMAPHORES = ["id0", "id1", "pk", "wl", "pa", "pb", "pc", "pf", "pt", "off", "wc0", "wc1", "gs",
-              "ls1", "lsent", "csent", "la", "lv", "lw", "lp", "lm", "ld1", "ld2", "ld3", "pt3", "off3",
-              "xz", "hv", "hs",
-              "mm1", "mm2", "mm0", "mm3a", "mm3b", "ev1", "ev2", "ev0", "ev3a", "ev3b",
-              "st1", "st2", "st0", "st3a", "st3b"]
-SEMAPHORES += ["%s%d" % (n, k) for n in ("wi", "we", "wv", "wd", "qw", "xc", "qx", "xl", "xf", "xe") for k in range(NR)]
+SEMAPHORES = ["id0", "id1", "ln", "pk", "pk2", "lq", "la", "lv", "lw", "px", "pw", "pwt", "offw", "pf", "pt", "offx",
+              "ls1", "lsent", "csent", "xz", "mma", "mmb", "eva", "evb", "sta", "stb",
+              "exa", "exb", "qha", "qhb", "ara", "arb"]
+SEMAPHORES += ["%s%d" % (n, k) for n in ("wl", "cv", "wi", "we", "wg", "wv", "wd", "qw", "xc", "qx", "mm", "ev", "st", "gx", "bk", "ex")
+               for k in range(NR)]
+SEMAPHORES += ["xl%d" % n for n in range(16)]
 SEMAPHORES += ["%s%d" % (n, k) for n in ("lst", "arr") for k in range(1, NR)]
-SEMAPHORES += ["ga%d%d" % (k, t) for k in range(NR) if k != WIN for t in range(4)]
+SEMAPHORES += ["ga%d%d" % (k, t) for k in DMAS for t in range(4)]
 
 COPY = ActivationFunctionType.Copy
 AND, SHR, ADD, MULT = AluOpType.bitwise_and, AluOpType.arith_shift_right, AluOpType.add, AluOpType.mult
@@ -72,6 +89,7 @@ def rank_program(g, core, T, topo):
     S = T.sem
     cores = T.cores
     v, a, te, sy = g.vector, g.scalar, g.tensor, g.sync
+    last = CFG["last"]
 
     def direct(k):
         return sum(1 for r in range(NR)
@@ -79,7 +97,6 @@ def rank_program(g, core, T, topo):
     steps = [0] + sorted(range(1, NR), key=direct)
     to = [(me + steps[k]) % NR for k in range(NR)]
     frm = [(me - steps[k]) % NR for k in range(NR)]
-    worder = [1, 0, 2, 3]
 
     def dst(r):
         rid, pid, _ = topo.addr(cores[r])
@@ -89,264 +106,265 @@ def rank_program(g, core, T, topo):
         return sum(1 << e for e in engs)
 
     off_chip = topo.engines(core, cores[frm[1]])
-    la, lb, lc = off_chip[0:4], off_chip[4:6], off_chip[6:8]
+    lengs = {1: off_chip[0:4], 2: off_chip[4:6], 3: off_chip[6:8]}
+    narr = 2 * len(off_chip)
+
+    def ycols(k, lo=0, hi=XC):
+        return slice(XC * frm[k] + lo, XC * frm[k] + hi)
+
+    def move(e, out, src):
+        return v.tensor_copy(out, src) if e is v else a.activation(out, src, COPY)
 
     sy.dma_start(T.pk[:], T.pick[:]).then_inc(S.pk, 16)
-    sy.dma_start(T.wb[:], T.w[:]).then_inc(S.wl, 16)
+    for q in range(4):
+        a.dma_start(T.pk2[32 * q:32 * q + 32, :], T.pick[q:128:4, :]).then_inc(S.pk2, 16)
+    for q in range(4):
+        a.dma_start(T.lq[32 * q:32 * q + 32], T.pick[:]).then_inc(S.lq, 16)
+    for b in range(4):
+        sy.dma_start(T.wb[:, 512 * b:512 * b + 512], T.w[512 * b:512 * b + 512, :]).then_inc(S["wl%d" % b], 16)
     for n in range(16):
         z, q = n // 4, n % 4
-        if n == 2:
-            sy.wait_ge(S.ls1, len(la))
-        if q == 0 and z >= 2:
-            sy.wait_ge(S["xl%d" % (z - 2)], 64)
+        if n >= CFG["depth"]:
+            sy.wait_ge(S["xl%d" % (n - CFG["depth"])], 16)
         sy.dma_start(T.xb[32 * q:32 * q + 32, 2048 * z:2048 * z + 2048],
-                     T.x[512 * z:512 * z + 512, 128 * q:128 * q + 128]).then_inc(S["xl%d" % z], 16)
+                     T.x[512 * z:512 * z + 512, 128 * q:128 * q + 128]).then_inc(S["xl%d" % n], 16)
 
     v.memset(T.ones[:], 1.0).then_inc(S.id0, 1)
-    v.wait_ge(S.pk, 16)
-    v.tensor_scalar(T.plo[:], T.pk[:], 15, None, AND).then_inc(S.pa, 1)
-    v.tensor_scalar(T.phi[:], T.pk[:], 4, None, SHR).then_inc(S.pb, 1)
-    v.wait_ge(S.pa, 1)
-    v.tensor_scalar(T.pls[:], T.plo[:], 128, None, MULT).then_inc(S.pc, 1)
-    v.wait_ge(S.pb, 1)
-    v.wait_ge(S.pc, 1)
-    for q in range(8):
-        v.tensor_tensor(T.pf[:, 16 * q:16 * q + 16], T.pls[:], T.phi[:], ADD).then_inc(S.pf, 1)
-    v.wait_ge(S.wl, 16)
-    for h in range(2):
-        v.tensor_copy(T.wf[:, 1024 * h:1024 * h + 1024], T.wb[:, 1024 * h:1024 * h + 1024]).then_inc(S["wc%d" % h], 1)
-    v.wait_ge(S.pt, 1)
-    v.tensor_copy(T.offs[:], T.ps_p[:, 0:128]).then_inc(S.off, 1)
-    li = T["li%d" % WIN]
-    v.wait_ge(S["lst%d" % WIN], len(lc))
-    v.tensor_scalar(T.lu[:], li[:], 5, 48, SHR, AND).then_inc(S.la, 1)
-    v.tensor_scalar(T.lb[:], li[:], 15, None, AND).then_inc(S.la, 1)
-    v.tensor_scalar(T.lc[:], li[:], 4, 31, SHR, AND).then_inc(S.la, 1)
-    v.wait_ge(S.la, 3)
-    v.tensor_tensor(T.lv[:], T.lu[:], T.lb[:], ADD).then_inc(S.lv, 1)
-    v.wait_ge(S.lv, 1)
-    v.tensor_scalar(T.lw[:], T.lv[:], 128, None, MULT).then_inc(S.lw, 1)
-    v.wait_ge(S.lw, 1)
-    v.tensor_tensor(T.lp[:], T.lw[:], T.lc[:], ADD).then_inc(S.lp, 1)
-    v.wait_ge(S.lp, 1)
-    for m in range(4):
-        v.tensor_scalar(T.pf3[:, 4 * m:4 * m + 4], T.lp[:], 32 * m, None, ADD).then_inc(S.lm, 1)
-    v.wait_ge(S.lm, 4)
-    v.tensor_copy(T.pf3[:, 16:32], T.pf3[:, 0:16]).then_inc(S.ld1, 1)
-    v.wait_ge(S.ld1, 1)
-    v.tensor_copy(T.pf3[:, 32:64], T.pf3[:, 0:32]).then_inc(S.ld2, 1)
-    v.wait_ge(S.ld2, 1)
-    v.tensor_copy(T.pf3[:, 64:128], T.pf3[:, 0:64]).then_inc(S.ld3, 1)
-
-    for b in range(4):
-        a.wait_ge(S["wi%d" % b], 4)
-        o = 512 * (b % 2)
-        a.activation(T.wtr[:, 512 * b:512 * b + 512], T.ps_w[:, o:o + 512], COPY).then_inc(S["we%d" % b], 1)
-    a.wait_ge(S.off, 1)
-    for b in range(4):
-        a.wait_ge(S["we%d" % b], 1)
-    a.activation(T.wg[:], T.wtr[:].indirect(T.offs[:, 0:128]), COPY).then_inc(S.gs, 1)
-
+    g.iota(T.lanes[:], [[0, 8], [32, 4]], 0, 0, allow_small_or_imprecise_dtypes=True).then_inc(S.ln, 1)
+    g.wait_ge(S.id0, 1)
+    g.affine_select(T.ident[:], T.ones[:], [[-1, 128]], AluOpType.is_equal, 0.0, 0, 1).then_inc(S.id1, 1)
     te.wait_ge(S.id1, 1)
-    te.wait_ge(S.pf, 8)
-    te.transpose(T.ps_p[:, 0:128], T.pf[:], T.ident[:]).then_inc(S.pt, 1)
-    for b in range(4):
-        if b % 2 == 0:
-            te.wait_ge(S["wc%d" % (b // 2)], 1)
-        if b >= 2:
-            te.wait_ge(S["we%d" % (b - 2)], 1)
-        for i in range(4):
-            c = 4 * b + i
-            o = 512 * (b % 2) + 128 * i
-            te.transpose(T.ps_w[:, o:o + 128], T.wf[:, 128 * c:128 * c + 128], T.ident[:]).then_inc(S["wi%d" % b], 1)
-    te.wait_ge(S.off, 1)
-    te.wait_ge(S.ld3, 1)
-    te.transpose(T.ps_p[:, 128:256], T.pf3[:], T.ident[:]).then_inc(S.pt3, 1)
 
-    def wturn(n):
-        k, o = worder[n], 512 * (n % 2)
-        if n >= 2:
-            te.wait_ge(S["wd%d" % worder[n - 2]], 1)
-        for t in range(4):
-            te.transpose(T.ps_w[:, o + t:o + 512:4], T.wg[:, 4 * frm[k] + t:2048:16], T.ident[:]).then_inc(S["wv%d" % k], 1)
+    def v_pos():
+        v.wait_ge(S.pk2, 64)
+        v.tensor_scalar(T.lu[:], T.pk2[:], 5, 48, SHR, AND).then_inc(S.la, 1)
+        v.tensor_scalar(T.lb[:], T.pk2[:], 15, None, AND).then_inc(S.la, 1)
+        v.tensor_scalar(T.lc[:], T.pk2[:], 4, 31, SHR, AND).then_inc(S.la, 1)
+        v.wait_ge(S.la, 3)
+        v.tensor_tensor(T.lv[:], T.lu[:], T.lb[:], ADD).then_inc(S.lv, 1)
+        v.wait_ge(S.lv, 1)
+        v.tensor_scalar(T.lw[:], T.lv[:], 128, None, MULT).then_inc(S.lw, 1)
+        v.wait_ge(S.lw, 1)
+        v.tensor_tensor(T.px[:], T.lw[:], T.lc[:], ADD).then_inc(S.px, 1)
 
-    def wevac(n):
-        k, o = worder[n], 512 * (n % 2)
-        a.wait_ge(S["wv%d" % k], 4)
-        a.activation(T["wt%d" % k][:], T.ps_w[:, o:o + 512], COPY).then_inc(S["wd%d" % k], 1)
+    def v_woff():
+        v.wait_ge(S.lq, 64)
+        for s in range(NR):
+            for d in range(2):
+                o = 32 * s + 16 * d
+                v.tensor_copy(T.pw[:, o:o + 16], T.lq[:, :, 4 * s:4 * s + 4]).then_inc(S.pw, 1)
+        v.wait_ge(S.pw, 8)
+        v.transpose(T.pwt[:], T.pw[:]).then_inc(S.pwt, 1)
+        v.wait_ge(S.pwt, 1)
+        v.tensor_copy(T.offw[:], T.pwt[:]).then_inc(S.offw, 1)
 
-    te.wait_ge(S.gs, 1)
-    wturn(0)
-    wturn(1)
-    te.wait_ge(S.hv, 1)
-    te.wait_ge(S.hs, 1)
-    for m in range(4):
-        if m >= 2:
-            te.wait_ge(S["xe%d" % (m - 2)], 1)
-        o = 512 * (m % 2)
-        for t in range(4):
-            te.transpose(T.ps_x[:, o + t:o + 512:4], T.xg[:, 4 * m + t:2048:16], T.ident[:]).then_inc(S["xf%d" % m], 1)
-    wturn(2)
-    wturn(3)
+    def v_turn(z):
+        for q in range(4):
+            v.wait_ge(S["xl%d" % (4 * z + q)], 16)
+        v.transpose(T.xv[:, 2048 * z:2048 * z + 2048], T.xb[:, 2048 * z:2048 * z + 2048]).then_inc(S.xz, 1)
 
-    a.wait_ge(S.off3, 1)
-    a.wait_ge(S.xz, 4)
-    a.activation(T.xg[:, 1024:2048], T.xv[:].indirect(T.offs3[:, 64:128]), COPY).then_inc(S.hs, 1)
-    wevac(0)
-    wevac(1)
-    for m in range(4):
-        a.wait_ge(S["xf%d" % m], 4)
-        o = 512 * (m % 2)
-        a.activation(T.x3[:, :, 128 * m:128 * m + 128], T.ps_x[:, o:o + 512], COPY).then_inc(S["xe%d" % m], 1)
-    wevac(2)
-    wevac(3)
+    def v_pf():
+        v.wait_ge(S.ln, 1)
+        for n, k in enumerate(WINS):
+            v.wait_ge(S["lst%d" % k], len(lengs[k]))
+            for t in range(4):
+                v.tensor_scalar(T.pf[:, 128 * n + t:128 * n + 128:4], T.lanes[:], T["li%d" % k][:, t:t + 1], None,
+                                ADD).then_inc(S.pf, 1)
 
-    def xcopy(k, t):
-        v.wait_ge(S["ga%d%d" % (k, t)], 16)
-        v.tensor_copy(T["xt%d" % k][:, t:2048:4], T["xs%d" % k][:, 512 * t:512 * t + 512]).then_inc(S["xc%d" % k], 1)
+    def v_offs():
+        v.wait_ge(S.pt, 2)
+        v.tensor_copy(T.offx[:], T.ps_p[:, 0:256]).then_inc(S.offx, 1)
 
-    def xquant(k):
-        v.wait_ge(S["xc%d" % k], 4)
+    def gather_win(e, k, lo, hi):
+        if hi <= lo:
+            return
+        o = 128 * WINS.index(k)
+        e.wait_ge(S.offx, 1)
+        e.wait_ge(S.xz, 4)
+        move(e, T["xg%d" % k][:, 16 * lo:16 * hi], T.xv[:].indirect(T.offx[:, o + lo:o + hi])).then_inc(S["gx%d" % k], 1)
+
+    def v_back(k):
+        v.wait_ge(S["gx%d" % k], int(CFG["cut"][k] > 0) + int(CFG["cut"][k] < 128))
+        for m in range(4):
+            for t in range(4):
+                v.transpose(T["ex%d" % k][:, :, 128 * m + t:128 * m + 128:4],
+                            T["xg%d" % k][:, 4 * m + t:2048:16]).then_inc(S["bk%d" % k], 1)
+
+    def copy(e, k, t):
+        e.wait_ge(S["ga%d%d" % (k, t)], 16)
+        move(e, T["xt%d" % k][:, t:2048:4], T["xs%d" % k][:, 512 * t:512 * t + 512]).then_inc(S["xc%d" % k], 1)
+
+    def v_quant(k):
+        if k in WINS:
+            v.wait_ge(S["ex%d" % k], 64)
+        else:
+            v.wait_ge(S["xc%d" % k], 4)
         v.quantize_mx(T["xq%d" % k][:], T["xp%d" % k][:], T["xt%d" % k][:]).then_inc(S["qx%d" % k], 1)
 
-    def wquant(n):
-        k = worder[n]
+    def v_quant_half(h):
+        v.wait_ge(S["ex" + "ab"[h]], 32)
+        c = slice(256 * h, 256 * h + 256)
+        v.quantize_mx(T["xq%d" % last][:, c], T["xp%d" % last][:, c],
+                      T["xt%d" % last][:, 1024 * h:1024 * h + 1024]).then_inc(S["qh" + "ab"[h]], 1)
+
+    def v_wquant(k):
         v.wait_ge(S["wd%d" % k], 1)
         v.quantize_mx(T["wq%d" % k][:], T["wp%d" % k][:], T["wt%d" % k][:]).then_inc(S["qw%d" % k], 1)
 
-    def xturn(z):
-        v.wait_ge(S["xl%d" % z], 64)
-        v.transpose(T.xv[:, 2048 * z:2048 * z + 2048], T.xb[:, 2048 * z:2048 * z + 2048]).then_inc(S.xz, 1)
+    def yhalf(e, h):
+        n = "ab"[h]
+        e.wait_ge(S["mm" + n], 1)
+        move(e, T.ys[:, ycols(last, 256 * h, 256 * h + 256)], T.ps_y[:, 1536 * h:1536 * h + 256]).then_inc(S["ev" + n], 1)
 
-    xturn(0)
-    v.wait_ge(S.pt3, 1)
-    v.tensor_copy(T.offs3[:], T.ps_p[:, 128:256]).then_inc(S.off3, 1)
-    xturn(1)
-    xcopy(1, 0)
-    xcopy(1, 1)
-    xcopy(1, 2)
-    xturn(2)
-    xcopy(1, 3)
-    xquant(1)
-    xturn(3)
-    v.wait_ge(S.off3, 1)
-    v.wait_ge(S.xz, 4)
-    v.tensor_copy(T.xg[:, 0:1024], T.xv[:].indirect(T.offs3[:, 0:64])).then_inc(S.hv, 1)
-    for t in range(4):
-        xcopy(2, t)
-    xquant(2)
-    for m in range(4):
-        v.wait_ge(S["xe%d" % m], 1)
-    for q in range(4):
-        v.quantize_mx(T["xq%d" % WIN][:, 128 * q:128 * q + 128], T["xp%d" % WIN][:, 128 * q:128 * q + 128],
-                      T.x3[:, q, :]).then_inc(S["qx%d" % WIN], 1)
-    wquant(0)
-    wquant(1)
-    for t in range(4):
-        xcopy(0, t)
-    xquant(0)
-    wquant(2)
-    wquant(3)
+    worder = [int(n[2]) for n in CFG["t"] if n.startswith("wb")]
+    morder = [int(n[2]) for n in CFG["t"] if n.startswith("mm")]
 
-    g.wait_ge(S.id0, 1)
-    g.affine_select(T.ident[:], T.ones[:], [[-1, 128]], AluOpType.is_equal, 0.0, 0, 1).then_inc(S.id1, 1)
+    def a_cv(b):
+        a.wait_ge(S["wl%d" % b], 16)
+        a.activation(T.wf[:, 512 * b:512 * b + 512], T.wb[:, 512 * b:512 * b + 512], COPY).then_inc(S["cv%d" % b], 1)
 
-    def listmove(k, engs):
+    def a_we(b):
+        a.wait_ge(S["wi%d" % b], 4)
+        o = 512 * (b % 3)
+        a.activation(T.wtr[:, 512 * b:512 * b + 512], T.ps_w[:, o:o + 512], COPY).then_inc(S["we%d" % b], 1)
+
+    def w_gather(e, k):
+        e.wait_ge(S.offw, 1)
+        for b in range(4):
+            e.wait_ge(S["we%d" % b], 1)
+        s = frm[k]
+        move(e, T.wg[:, 512 * k:512 * k + 512], T.wtr[:].indirect(T.offw[:, 32 * s:32 * s + 32])).then_inc(S["wg%d" % k], 1)
+
+    def wbank(k):
+        return 512 * ((worder.index(k) + 1) % 3)
+
+    def w_down(e, k):
+        e.wait_ge(S["wv%d" % k], 4)
+        move(e, T["wt%d" % k][:], T.ps_w[:, wbank(k):wbank(k) + 512]).then_inc(S["wd%d" % k], 1)
+
+    def ybank(k):
+        return 512 * morder.index(k)
+
+    def y_out(e, k):
+        e.wait_ge(S["mm%d" % k], 1)
+        move(e, T.ys[:, ycols(k)], T.ps_y[:, ybank(k):ybank(k) + 512]).then_inc(S["ev%d" % k], 1)
+
+    def a_yb():
+        yhalf(a, 1)
+        a.wait_ge(S.evb, 1)
+        a.dma_start(T.y[:, ycols(last, 256, 512)], T.ys[:, ycols(last, 256, 512)]).then_inc(S.stb, 16)
+        a.wait_ge(S.stb, 16)
+
+    def t_wf(b):
+        te.wait_ge(S["cv%d" % b], 1)
+        if b >= 3:
+            te.wait_ge(S["we%d" % (b - 3)], 1)
+        o = 512 * (b % 3)
+        for i in range(4):
+            c = 4 * b + i
+            te.transpose(T.ps_w[:, o + i:o + 512:4], T.wf[:, 128 * c:128 * c + 128], T.ident[:]).then_inc(S["wi%d" % b], 1)
+
+    def t_offs():
+        te.wait_ge(S.pf, 8)
+        for n in range(2):
+            te.transpose(T.ps_p[:, 128 * n:128 * n + 128], T.pf[:, 128 * n:128 * n + 128], T.ident[:]).then_inc(S.pt, 1)
+
+    def t_wb(k):
+        te.wait_ge(S["wg%d" % k], 1)
+        n = worder.index(k)
+        if n >= 3:
+            te.wait_ge(S["wd%d" % worder[n - 3]], 1)
+        o = wbank(k)
+        for t in range(4):
+            te.transpose(T.ps_w[:, o + t:o + 512:4], T.wg[:, 512 * k + t:512 * k + 512:4], T.ident[:]).then_inc(S["wv%d" % k], 1)
+
+    def t_mm(k):
+        te.wait_ge(S["qw%d" % k], 1)
+        wq, wp = T["wq%d" % k][:], T["wp%d" % k][:]
+        xq, xp = (T["rq%d" % k], T["rp%d" % k]) if k else (T.xq0, T.xp0)
+        if k != last:
+            if k:
+                te.wait_ge(S["arr%d" % k], narr)
+            else:
+                te.wait_ge(S.qx0, 1)
+            o = ybank(k)
+            te.matmul_mx(T.ps_y[:, o:o + 512], wq, wp, xq[:], xp[:], True, True).then_inc(S["mm%d" % k], 1)
+            return
+        te.wait_ge(S["ev%d" % morder[0]], 1)
+        for h in range(2):
+            c = slice(256 * h, 256 * h + 256)
+            te.wait_ge(S["ar" + "ab"[h]], narr)
+            te.matmul_mx(T.ps_y[:, 1536 * h:1536 * h + 256], wq, wp, xq[:, c], xp[:, c], True, True).then_inc(S["mm" + "ab"[h]], 1)
+
+    def listmove(k):
         s = frm[k]
         rid, pid = dst(s)
-        return RemoteDMATransfer(dst_ids=[DstId(rid=rid, pnc=pid)], dma_engine_mask=bits(engs),
-                                 remote_sem=S["lst%d" % k],
-                                 srcs=[T.pk[:, 4 * s:4 * s + 4]], dsts=[T["li%d" % k][:]])
+        src = T.px if k in WINS else T.pk
+        return RemoteDMATransfer(dst_ids=[DstId(rid=rid, pnc=pid)], dma_engine_mask=bits(lengs[k]),
+                                 remote_sem=S["lst%d" % k], srcs=[src[:, 4 * s:4 * s + 4]], dsts=[T["li%d" % k][:]])
+
+    def g_l1():
+        g.wait_ge(S.pk, 16)
+        g.remote_dma_fused([listmove(1)], local_sem=S.ls1)
+
+    def g_l23():
+        g.wait_ge(S.px, 1)
+        g.remote_dma_fused([listmove(2), listmove(3)], local_sem=S.lsent)
 
     def gather(k, t):
         idx = T["li%d" % k][:, t:t + 1] if k else T.pk[:, 4 * me + t:4 * me + t + 1]
         g.indirect_dma_start(T["xs%d" % k][:, 512 * t:512 * t + 512], None, T.x[:],
                              IndirectOffsetOnAxis(ap=idx, axis=0), bounds_check=ROWS - 1).then_inc(S["ga%d%d" % (k, t)], 16)
 
-    def send_fused(k):
+    def send(k, ready, arrived, c):
         e = topo.engines(core, cores[to[k]])
         rid, pid = dst(to[k])
-        parts = [e[0:2], e[2:4], e[4:6], e[6:7], e[7:8]]
-        tr = []
-        for i, p in enumerate(parts):
-            if i < 4:
-                src = T["xq%d" % k][:, 128 * i:128 * i + 128].bitcast(dt.uint8)
-                d = T["rq%d" % k][:, 128 * i:128 * i + 128].bitcast(dt.uint8)
-            else:
-                src, d = T["xp%d" % k][:], T["rp%d" % k][:]
-            tr.append(RemoteDMATransfer(dst_ids=[DstId(rid=rid, pnc=pid)], dma_engine_mask=bits(p),
-                                        remote_sem=S["arr%d" % k], srcs=[src], dsts=[d]))
-        g.remote_dma_fused(tr, local_sem=S.csent)
-        return sum(len(p) for p in parts)
+        g.wait_ge(ready, 1)
+        g.remote_dma(T["rq%d" % k][:, c].bitcast(dt.uint8), T["xq%d" % k][:, c].bitcast(dt.uint8),
+                     arrived, S.csent, pid, rid, bits(e))
+        g.remote_dma(T["rp%d" % k][:, c], T["xp%d" % k][:, c], arrived, S.csent, pid, rid, bits(e))
 
-    def send_two(k):
-        e = topo.engines(core, cores[to[k]])
-        rid, pid = dst(to[k])
-        g.remote_dma(T["rq%d" % k][:].bitcast(dt.uint8), T["xq%d" % k][:].bitcast(dt.uint8),
-                     S["arr%d" % k], S.csent, pid, rid, bits(e))
-        g.remote_dma(T["rp%d" % k][:], T["xp%d" % k][:], S["arr%d" % k], S.csent, pid, rid, bits(e))
-        return 2 * len(e)
+    def send_whole(k):
+        send(k, S["qx%d" % k], S["arr%d" % k], slice(0, XC))
 
-    g.wait_ge(S.pk, 16)
-    g.remote_dma_fused([listmove(1, la)], local_sem=S.ls1)
-    gather(0, 0)
-    g.remote_dma_fused([listmove(2, lb), listmove(3, lc)], local_sem=S.lsent)
-    gather(0, 1)
-    g.wait_ge(S.lst1, len(la))
-    for t in range(4):
-        gather(1, t)
-    g.wait_ge(S.lst2, len(lb))
-    for t in range(3):
-        gather(2, t)
-    g.wait_ge(S.qx1, 1)
-    n1 = send_fused(1)
-    gather(2, 3)
-    gather(0, 2)
-    gather(0, 3)
-    g.wait_ge(S.qx2, 1)
-    n2 = send_two(2)
-    g.wait_ge(S["qx%d" % WIN], 4)
-    n3 = send_two(WIN)
-    g.wait_ge(S.lsent, len(lb) + len(lc))
-    g.wait_ge(S.csent, n1 + n2 + n3)
+    def send_half(h):
+        send(last, S["qh" + "ab"[h]], S["ar" + "ab"[h]], slice(256 * h, 256 * h + 256))
 
-    bank = {1: 0, 0: 512, 2: 1024}
-    narr = {1: n1, 2: n2}
-    for k in worder[:3]:
-        o = bank[k]
-        te.wait_ge(S["qw%d" % k], 1)
-        if k:
-            te.wait_ge(S["arr%d" % k], narr[k])
-            xq, xp = T["rq%d" % k], T["rp%d" % k]
-        else:
-            te.wait_ge(S.qx0, 1)
-            xq, xp = T.xq0, T.xp0
-        te.matmul_mx(T.ps_y[:, o:o + 512], T["wq%d" % k][:], T["wp%d" % k][:], xq[:], xp[:], True, True).then_inc(S["mm%d" % k], 1)
-    te.wait_ge(S.qw3, 1)
-    te.wait_ge(S.ev1, 1)
-    te.wait_ge(S.ev0, 1)
-    te.wait_ge(S.arr3, n3)
-    te.matmul_mx(T.ps_y[:, 0:256], T.wq3[:], T.wp3[:], T.rq3[:, 0:256], T.rp3[:, 0:256], True, True).then_inc(S.mm3a, 1)
-    te.matmul_mx(T.ps_y[:, 512:768], T.wq3[:], T.wp3[:], T.rq3[:, 256:512], T.rp3[:, 256:512], True, True).then_inc(S.mm3b, 1)
+    def s_ex(k):
+        sy.wait_ge(S["bk%d" % k], 16)
+        for q in range(4):
+            sem = S["ex%d" % k] if k != last else S["ex" + "ab"[q // 2]]
+            sy.dma_start(T["xt%d" % k][:, 512 * q:512 * q + 512], T["ex%d" % k][32 * q:32 * q + 32]).then_inc(sem, 16)
 
-    def ycols(k, lo=0, hi=XC):
-        b = XC * frm[k]
-        return slice(b + lo, b + hi)
-
-    for k in worder[:3]:
-        o = bank[k]
-        a.wait_ge(S["mm%d" % k], 1)
-        a.activation(T.ys[:, ycols(k)], T.ps_y[:, o:o + 512], COPY).then_inc(S["ev%d" % k], 1)
+    def s_st(k):
         sy.wait_ge(S["ev%d" % k], 1)
         sy.dma_start(T.y[:, ycols(k)], T.ys[:, ycols(k)]).then_inc(S["st%d" % k], 16)
-    v.wait_ge(S.mm3a, 1)
-    v.tensor_copy(T.ys[:, ycols(3, 0, 256)], T.ps_y[:, 0:256]).then_inc(S.ev3a, 1)
-    sy.wait_ge(S.ev3a, 1)
-    sy.dma_start(T.y[:, ycols(3, 0, 256)], T.ys[:, ycols(3, 0, 256)]).then_inc(S.st3a, 16)
-    a.wait_ge(S.mm3b, 1)
-    a.activation(T.ys[:, ycols(3, 256, 512)], T.ps_y[:, 512:768], COPY).then_inc(S.ev3b, 1)
-    a.wait_ge(S.ev3b, 1)
-    a.dma_start(T.y[:, ycols(3, 256, 512)], T.ys[:, ycols(3, 256, 512)]).then_inc(S.st3b, 16)
-    for n in ("st1", "st2", "st0", "st3a"):
-        sy.wait_ge(S[n], 16)
-    a.wait_ge(S.st3b, 16)
+
+    def s_sta():
+        sy.wait_ge(S.eva, 1)
+        sy.dma_start(T.y[:, ycols(last, 0, 256)], T.ys[:, ycols(last, 0, 256)]).then_inc(S.sta, 16)
+
+    def play(order, plain, numbered):
+        for n in order:
+            if n in plain:
+                plain[n]()
+            else:
+                head = n.rstrip("0123456789")
+                numbered[head](*[int(c) for c in n[len(head):]])
+
+    play(CFG["v"], {"pos": v_pos, "woff": v_woff, "pf": v_pf, "offs": v_offs, "ya": lambda: yhalf(v, 0)},
+         {"turn": v_turn, "g": lambda k: gather_win(v, k, 0, CFG["cut"][k]), "back": v_back, "c": lambda k, t: copy(v, k, t),
+          "q": v_quant, "qh": v_quant_half, "wq": v_wquant, "y": lambda k: y_out(v, k), "wg": lambda k: w_gather(v, k),
+          "wd": lambda k: w_down(v, k)})
+    play(CFG["a"], {"yb": a_yb},
+         {"cv": a_cv, "we": a_we, "g": lambda k: gather_win(a, k, CFG["cut"][k], 128), "wg": lambda k: w_gather(a, k),
+          "wd": lambda k: w_down(a, k), "c": lambda k, t: copy(a, k, t), "y": lambda k: y_out(a, k)})
+    play(CFG["t"], {"offs": t_offs}, {"wf": t_wf, "wb": t_wb, "mm": t_mm})
+    play(CFG["g"], {"l1": g_l1, "l23": g_l23, "wl": lambda: g.wait_ge(S.lst1, len(lengs[1]))},
+         {"ga": gather, "s": send_whole, "sh": send_half})
+    play(CFG["s"], {"sta": s_sta}, {"ex": s_ex, "st": s_st})
+    g.wait_ge(S.ls1, len(lengs[1]))
+    g.wait_ge(S.lsent, len(lengs[2]) + len(lengs[3]))
+    g.wait_ge(S.csent, 4 * narr)
+    for k in range(NR):
+        sy.wait_ge(S["st%d" % k] if k != last else S.sta, 16)

@@ -7,37 +7,57 @@ WC = 128
 ROWS = 2048
 WINS = (2, 3)
 DMAS = (1, 0)
+LAST = 3
 
 CFG = {
-    "depth": 6,
-    "cut": {2: 64, 3: 40},
-    "last": 3,
-    "v": ["pos", "woff", "turn0", "turn1", "pf", "turn2", "offs", "turn3", "g2", "back2", "g3", "back3", "q1", "q2", "wq1",
-          "c00", "c01", "qh0", "qh1", "wq2", "c02", "wq0", "wq3", "c03", "q0", "ya"],
-    "a": ["cv0", "cv1", "we0", "cv2", "we1", "cv3", "we2", "we3", "wg1", "wg2", "g2", "g3", "c10", "c11", "c12", "c13",
-          "wd1", "wg0", "wd2", "wg3", "wd0", "wd3", "y1", "y2", "y0", "yb"],
-    "t": ["wf0", "wf1", "wf2", "wf3", "offs", "wb1", "wb2", "wb0", "wb3", "mm1", "mm2", "mm0", "mm3"],
-    "g": ["l1", "l23", "ga00", "wl", "ga10", "ga11", "ga12", "ga13", "ga01", "ga02", "s1", "s2", "ga03", "sh0", "sh1"],
-    "s": ["ex2", "ex3", "st1", "st2", "st0", "sta"],
+    "depth": 7,
+    "pieces": (),
+    "pe": (21, 30),
+    "nz": 4,
+    "gfirst": False,
+    "wide": True,
+    "v": ["pos", "cv1", "wpos", "wdup", "turn0", "woff", "turn1", "pf", "turn2", "offs", "turn3", "g21:0:44", "g20:0:24",
+          "c10", "back20", "c12", "c13", "q1", "g31:0:40", "back31", "qu21", "qu20", "wd2", "c01", "wd1", "wq1", "qu30",
+          "wd0", "wq2", "qu31", "c00", "c03", "wq0", "q0", "y2", "wq3", "yu", "yh0"],
+    "a": ["pa0", "pa1", "pa2", "pa3", "lq0", "lq1", "lq2", "lq3", "cv0", "cv2", "we0", "cv3", "we1", "we2", "we3", "wg2", "wg1",
+          "g20:24:64", "g21:44:64", "c11", "g30:0:64", "xe210", "g31:40:64", "xe211", "wg0", "xe300", "xe301", "wg3",
+          "c02", "y1", "wd3", "y0", "yh1"],
+    "t": ["wf0", "wf1", "wf2", "wf3", "offs", "wb2", "wb1", "xb21", "xb30", "wb0", "mm1", "wb3", "mm2", "mm0", "mu", "mh"],
+    "g": ["l1", "ga00", "l23", "ga10", "ga11", "ga12", "ga13", "ga01", "s1", "ga02", "s2", "ga03", "sh30", "sh31", "go"],
+    "s": ["pa4", "w0", "w1", "w2", "w3", "x0:16", "ex20", "ex31", "go", "st1", "st2", "st0", "sth"],
 }
 
 SCRATCH = {
     "pk": ("sbuf", [128, 16], "int32"),
-    "pk2": ("sbuf", [128, 16], "int32"),
     "lq": ("sbuf", [128, 4, 16], "int32"),
-    "lu": ("sbuf", [128, 16], "int32"),
-    "lb": ("sbuf", [128, 16], "int32"),
-    "lc": ("sbuf", [128, 16], "int32"),
-    "lv": ("sbuf", [128, 16], "int32"),
-    "lw": ("sbuf", [128, 16], "int32"),
-    "px": ("sbuf", [128, 16], "float32"),
+    "pa": ("sbuf", [128, 6, 8], "int32"),
+    "lu": ("sbuf", [128, 6, 8], "int32"),
+    "lb": ("sbuf", [128, 6, 8], "int32"),
+    "lc": ("sbuf", [128, 6, 8], "int32"),
+    "lv": ("sbuf", [128, 6, 8], "int32"),
+    "lw": ("sbuf", [128, 6, 8], "int32"),
+    "px": ("sbuf", [128, 6, 8], "float32"),
+    "pxu": ("sbuf", [128, 2, 8], "uint16"),
+    "pxs": ("sbuf", [128, 4], "float32"),
+    "lp": ("sbuf", [128, 4], "float32"),
+    "wu": ("sbuf", [128, 4, 16], "int32"),
+    "wx": ("sbuf", [128, 4, 16], "int32"),
+    "wc": ("sbuf", [128, 4, 16], "int32"),
+    "wy": ("sbuf", [128, 4, 16], "int32"),
+    "wz": ("sbuf", [128, 4, 16], "int32"),
+    "wpos": ("sbuf", [128, 4, 16], "float32"),
+    "wn": ("sbuf", [128, 16, 128], "bfloat16"),
+    "wv": ("sbuf", [128, 4, 512], "bfloat16"),
     "pw": ("sbuf", [128, 128], "float32"),
     "pwt": ("sbuf", [128, 128], "float32"),
     "offw": ("sbuf", [128, 128], "uint16"),
     "lanes": ("sbuf", [128, 32], "float32"),
-    "pf": ("sbuf", [128, 256], "float32"),
-    "offx": ("sbuf", [128, 256], "uint16"),
+    "pf": ("sbuf", [128, 2, 16, 8], "float32"),
+    "pfo": ("sbuf", [128, 2, 8, 16], "float32"),
+    "offx": ("sbuf", [128, 512], "uint16"),
     "ones": ("sbuf", [128, 128], "float32"),
+    "cols": ("sbuf", [128, 128], "float32"),
+    "parts": ("sbuf", [128, 128], "float32"),
     "ident": ("sbuf", [128, 128], "float32"),
     "wb": ("sbuf", [128, 2048], "bfloat16"),
     "wf": ("sbuf", [128, 2048], "float32"),
@@ -45,35 +65,42 @@ SCRATCH = {
     "wg": ("sbuf", [128, 2048], "float32"),
     "xb": ("sbuf", [128, 8192], "bfloat16"),
     "xv": ("sbuf", [128, 8192], "bfloat16"),
-    "ys": ("sbuf", [128, 2048], "float32"),
-    "ps_p": ("psum", [128, 512], "float32"),
-    "ps_w": ("psum", [128, 1536], "float32"),
+    "xo": ("sbuf", [128, 1024], "float32"),
+    "ys": ("sbuf", [128, 16, 4, 32], "float32"),
+    "ps_w": ("psum", [128, 1024], "float32"),
+    "ps_x": ("psum", [128, 1024], "float32"),
     "ps_y": ("psum", [128, 2048], "float32"),
 }
 for _k in range(NR):
     if _k in WINS:
         SCRATCH["xg%d" % _k] = ("sbuf", [128, 2048], "bfloat16")
-        SCRATCH["ex%d" % _k] = ("sbuf", [128, 4, 512], "bfloat16")
-        SCRATCH["li%d" % _k] = ("sbuf", [128, 4], "float32")
+        SCRATCH["xf%d" % _k] = ("sbuf", [128, 2048], "float32")
+        for _h in range(2):
+            SCRATCH["xs%d%d" % (_k, _h)] = ("sbuf", [128, 4, 256], "bfloat16")
+        SCRATCH["li%d" % _k] = ("sbuf", [128, 8], "uint16")
     else:
         SCRATCH["xs%d" % _k] = ("sbuf", [128, 2048], "bfloat16")
         if _k:
             SCRATCH["li%d" % _k] = ("sbuf", [128, 4], "int32")
-    SCRATCH["xt%d" % _k] = ("sbuf", [128, 2048], "bfloat16")
+    SCRATCH["xt%d" % _k] = ("sbuf", [128, 2048] if _k in WINS else [128, 4, 512], "bfloat16")
+    if _k:
+        SCRATCH["rq%d" % _k] = ("sbuf", [128, XC], "float8_e4m3fn_x4")
+        SCRATCH["rp%d" % _k] = ("sbuf", [128, XC], "uint8")
     SCRATCH["xq%d" % _k] = ("sbuf", [128, XC], "float8_e4m3fn_x4")
     SCRATCH["xp%d" % _k] = ("sbuf", [128, XC], "uint8")
     SCRATCH["wt%d" % _k] = ("sbuf", [128, 512], "bfloat16")
     SCRATCH["wq%d" % _k] = ("sbuf", [128, WC], "float8_e4m3fn_x4")
     SCRATCH["wp%d" % _k] = ("sbuf", [128, WC], "uint8")
-    if _k:
-        SCRATCH["rq%d" % _k] = ("sbuf", [128, XC], "float8_e4m3fn_x4")
-        SCRATCH["rp%d" % _k] = ("sbuf", [128, XC], "uint8")
 
-SEMAPHORES = ["id0", "id1", "ln", "pk", "pk2", "lq", "la", "lv", "lw", "px", "pw", "pwt", "offw", "pf", "pt", "offx",
-              "ls1", "lsent", "csent", "xz", "mma", "mmb", "eva", "evb", "sta", "stb",
-              "exa", "exb", "qha", "qhb", "ara", "arb"]
-SEMAPHORES += ["%s%d" % (n, k) for n in ("wl", "cv", "wi", "we", "wg", "wv", "wd", "qw", "xc", "qx", "mm", "ev", "st", "gx", "bk", "ex")
-               for k in range(NR)]
+SEMAPHORES = ["id0", "id1", "id2", "id3", "go", "ln", "lq", "lq0", "pk", "pa", "la", "lv", "lw", "px", "pxu", "pw", "pwt",
+              "offw", "pf0", "pf1", "pf2", "pf3", "wpos", "wa", "wy", "wz", "pt", "offx", "ls1", "lsent", "csent", "xz",
+              "mu", "eu", "mh0", "mh1", "eh0", "eh1", "sh0", "sh1", "ar0", "ar1", "stu"]
+SEMAPHORES += ["%s%d" % (n, k) for n in ("wl", "cv", "wi", "we", "wg", "wv", "wd", "qw", "mm", "ev", "st") for k in range(NR)]
+SEMAPHORES += ["%s%d" % (n, k) for n in ("xc", "qx") for k in DMAS]
+SEMAPHORES += ["%s%d" % (n, k) for n in ("og", "ob", "oe", "pfo") for k in CFG["pieces"]]
+SEMAPHORES += ["pz", "lsp", "pxs"] if CFG["pieces"] else []
+SEMAPHORES += ["%s%d%d" % (n, kh, m) for n in ("xi", "xe") for kh in CFG["pe"] for m in range(2)]
+SEMAPHORES += ["%s%d%d" % (n, k, h) for n in ("gx", "bk", "ex", "qu") for k in WINS for h in range(2)]
 SEMAPHORES += ["xl%d" % n for n in range(16)]
 SEMAPHORES += ["%s%d" % (n, k) for n in ("lst", "arr") for k in range(1, NR)]
 SEMAPHORES += ["ga%d%d" % (k, t) for k in DMAS for t in range(4)]
@@ -89,7 +116,8 @@ def rank_program(g, core, T, topo):
     S = T.sem
     cores = T.cores
     v, a, te, sy = g.vector, g.scalar, g.tensor, g.sync
-    last = CFG["last"]
+    PIECES, PE, WEX = tuple(CFG["pieces"]), CFG["pe"], "wex" in CFG["a"]
+    nt = {k: 3 if k in PIECES else 4 for k in DMAS}
 
     def direct(k):
         return sum(1 for r in range(NR)
@@ -106,212 +134,432 @@ def rank_program(g, core, T, topo):
         return sum(1 << e for e in engs)
 
     off_chip = topo.engines(core, cores[frm[1]])
-    lengs = {1: off_chip[0:4], 2: off_chip[4:6], 3: off_chip[6:8]}
+    lengs = {1: off_chip[0:4], 2: off_chip[4:6], 3: off_chip[6:8], "p": off_chip[0:2]}
+    if CFG.get("wide"):
+        lengs = {1: off_chip[0:4], 2: off_chip[0:4], 3: off_chip[4:8]}
     narr = 2 * len(off_chip)
-
-    def ycols(k, lo=0, hi=XC):
-        return slice(XC * frm[k] + lo, XC * frm[k] + hi)
 
     def move(e, out, src):
         return v.tensor_copy(out, src) if e is v else a.activation(out, src, COPY)
 
     sy.dma_start(T.pk[:], T.pick[:]).then_inc(S.pk, 16)
-    for q in range(4):
-        a.dma_start(T.pk2[32 * q:32 * q + 32, :], T.pick[q:128:4, :]).then_inc(S.pk2, 16)
-    for q in range(4):
-        a.dma_start(T.lq[32 * q:32 * q + 32], T.pick[:]).then_inc(S.lq, 16)
-    for b in range(4):
-        sy.dma_start(T.wb[:, 512 * b:512 * b + 512], T.w[512 * b:512 * b + 512, :]).then_inc(S["wl%d" % b], 16)
-    for n in range(16):
-        z, q = n // 4, n % 4
-        if n >= CFG["depth"]:
-            sy.wait_ge(S["xl%d" % (n - CFG["depth"])], 16)
-        sy.dma_start(T.xb[32 * q:32 * q + 32, 2048 * z:2048 * z + 2048],
-                     T.x[512 * z:512 * z + 512, 128 * q:128 * q + 128]).then_inc(S["xl%d" % n], 16)
+    def load_pa(e, q):
+        if q < 4:
+            e.dma_start(T.pa[16 * q:16 * q + 16, 0:4, :], T.pick[q:128:4, :]).then_inc(S.pa, 16)
+        else:
+            e.dma_start(T.pa[64:128, 0:4, :], T.pick[:]).then_inc(S.pa, 16)
+
+    for n, k in enumerate(PIECES):
+        sy.dma_start(T.pa[0:32, 4 + n, :], T.pick[:, 4 * frm[k] + 2:4 * frm[k] + 4]).then_inc(S.pa, 16)
+    nq = 1 if CFG["gfirst"] is True else 0
+
+    def load_lq(e, q):
+        e.dma_start(T.lq[32 * q:32 * q + 32], T.pick[:]).then_inc(S.lq0 if e is g else S.lq, 16)
+
+    if nq:
+        load_lq(g, 0)
+
+    def load_w(e, b):
+        e.dma_start(T.wb[:, 512 * b:512 * b + 512], T.w[512 * b:512 * b + 512, :]).then_inc(S["wl%d" % b], 16)
+
+    if CFG["gfirst"] == "w":
+        load_w(g, 3)
+
+    NZ = CFG["nz"]
+    per = 4 * NZ // 16
+    zr, zc = ROWS // NZ, 8192 // NZ
+
+    def load_x(lo, hi):
+        for n in range(lo, hi):
+            z, q = n // 4, n % 4
+            if n % per == 0 and n // per >= CFG["depth"]:
+                sy.wait_ge(S["xl%d" % (n // per - CFG["depth"])], 16 * per)
+            sy.dma_start(T.xb[32 * q:32 * q + 32, zc * z:zc * z + zc],
+                         T.x[zr * z:zr * z + zr, 128 * q:128 * q + 128]).then_inc(S["xl%d" % (n // per)], 16)
 
     v.memset(T.ones[:], 1.0).then_inc(S.id0, 1)
-    g.iota(T.lanes[:], [[0, 8], [32, 4]], 0, 0, allow_small_or_imprecise_dtypes=True).then_inc(S.ln, 1)
-    g.wait_ge(S.id0, 1)
-    g.affine_select(T.ident[:], T.ones[:], [[-1, 128]], AluOpType.is_equal, 0.0, 0, 1).then_inc(S.id1, 1)
-    te.wait_ge(S.id1, 1)
+    v.wait_ge(S.id0, 1)
+    v.tensor_tensor_scan(T.cols[:], T.ones[:], T.ones[:], 0.0, MULT, ADD).then_inc(S.id1, 1)
+    for m in range(4 if PIECES else 0):
+        v.memset(T.lanes[:, m:32:4], 32.0 * m).then_inc(S.ln, 1)
+    v.wait_ge(S.id1, 1)
+    v.transpose(T.parts[:], T.cols[:]).then_inc(S.id2, 1)
+    if PIECES:
+        for part in (slice(32, 64), slice(64, 128)):
+            v.memset(T.pa[part, 4:6, :], 0).then_inc(S.pz, 1)
+    v.wait_ge(S.id2, 1)
+    for q in range(4):
+        part = slice(32 * q, 32 * q + 32)
+        v.tensor_scalar(T.ident[part, :], T.cols[part, :], T.parts[part, 32 * q:32 * q + 1], None,
+                        AluOpType.is_equal).then_inc(S.id3, 1)
+    te.wait_ge(S.id3, 4)
 
     def v_pos():
-        v.wait_ge(S.pk2, 64)
-        v.tensor_scalar(T.lu[:], T.pk2[:], 5, 48, SHR, AND).then_inc(S.la, 1)
-        v.tensor_scalar(T.lb[:], T.pk2[:], 15, None, AND).then_inc(S.la, 1)
-        v.tensor_scalar(T.lc[:], T.pk2[:], 4, 31, SHR, AND).then_inc(S.la, 1)
+        v.wait_ge(S.pa, 16 * (5 + len(PIECES)))
+        n = 4 + len(PIECES)
+        if PIECES:
+            v.wait_ge(S.pz, 2)
+        nb = zr // 32
+        v.tensor_scalar(T.lu[:, 0:n], T.pa[:, 0:n], 5, 64 - nb, SHR, AND).then_inc(S.la, 1)
+        v.tensor_scalar(T.lb[:, 0:n], T.pa[:, 0:n], nb - 1, None, AND).then_inc(S.la, 1)
+        v.tensor_scalar(T.lc[:, 0:n], T.pa[:, 0:n], nb.bit_length() - 1, 31, SHR, AND).then_inc(S.la, 1)
         v.wait_ge(S.la, 3)
-        v.tensor_tensor(T.lv[:], T.lu[:], T.lb[:], ADD).then_inc(S.lv, 1)
+        v.tensor_tensor(T.lv[:, 0:n], T.lu[:, 0:n], T.lb[:, 0:n], ADD).then_inc(S.lv, 1)
         v.wait_ge(S.lv, 1)
-        v.tensor_scalar(T.lw[:], T.lv[:], 128, None, MULT).then_inc(S.lw, 1)
+        v.tensor_scalar(T.lw[:, 0:n], T.lv[:, 0:n], 128, None, MULT).then_inc(S.lw, 1)
         v.wait_ge(S.lw, 1)
-        v.tensor_tensor(T.px[:], T.lw[:], T.lc[:], ADD).then_inc(S.px, 1)
+        v.tensor_tensor(T.px[:, 0:n], T.lw[:, 0:n], T.lc[:, 0:n], ADD).then_inc(S.px, 1)
+        v.wait_ge(S.px, 1)
+        for n, k in enumerate(WINS):
+            s = frm[k]
+            v.tensor_copy(T.pxu[:, n, :], T.px[:, s // 2:4:2, 4 * (s % 2):4 * (s % 2) + 4]).then_inc(S.pxu, 1)
+        if 1 in PIECES:
+            v.tensor_copy(T.pxs[:], T.px[:, 4 + PIECES.index(1), 1:8:2]).then_inc(S.pxs, 1)
 
-    def v_woff():
-        v.wait_ge(S.lq, 64)
+    def v_wpos():
+        v.wait_ge(S.lq, 16 * (4 - nq))
+        if nq:
+            v.wait_ge(S.lq0, 16)
+        if not WEX:
+            v.tensor_copy(T.wpos[:], T.lq[:]).then_inc(S.wpos, 1)
+            return
+        v.tensor_scalar(T.wu[:], T.lq[:], 5, 48, SHR, AND).then_inc(S.wa, 1)
+        v.tensor_scalar(T.wx[:], T.lq[:], 15, None, AND).then_inc(S.wa, 1)
+        v.tensor_scalar(T.wc[:], T.lq[:], 4, 31, SHR, AND).then_inc(S.wa, 1)
+        v.wait_ge(S.wa, 3)
+        v.tensor_tensor(T.wy[:], T.wu[:], T.wx[:], ADD).then_inc(S.wy, 1)
+        v.wait_ge(S.wy, 1)
+        v.tensor_scalar(T.wz[:], T.wy[:], 32, None, MULT).then_inc(S.wz, 1)
+        v.wait_ge(S.wz, 1)
+        v.tensor_tensor(T.wpos[:], T.wz[:], T.wc[:], ADD).then_inc(S.wpos, 1)
+
+    def w_dup(e):
+        e.wait_ge(S.wpos, 1)
         for s in range(NR):
             for d in range(2):
                 o = 32 * s + 16 * d
-                v.tensor_copy(T.pw[:, o:o + 16], T.lq[:, :, 4 * s:4 * s + 4]).then_inc(S.pw, 1)
+                move(e, T.pw[:, o:o + 16], T.wpos[:, :, 4 * s:4 * s + 4]).then_inc(S.pw, 1)
+
+    def v_wturn():
+        v.wait_ge(S.wl0, 16)
+        for m in range(4):
+            v.transpose(T.wv[:, m, :], T.wn[:, :, m:128:4]).then_inc(S.wi0, 1)
+
+    def a_wex():
+        a.wait_ge(S.wi0, 4)
+        for q in range(4):
+            a.dma_start(T.wtr[:, 512 * q:512 * q + 512], T.wv[32 * q:32 * q + 32]).then_inc(S.we0, 16)
+
+    def v_woff():
         v.wait_ge(S.pw, 8)
         v.transpose(T.pwt[:], T.pw[:]).then_inc(S.pwt, 1)
         v.wait_ge(S.pwt, 1)
         v.tensor_copy(T.offw[:], T.pwt[:]).then_inc(S.offw, 1)
 
-    def v_turn(z):
-        for q in range(4):
-            v.wait_ge(S["xl%d" % (4 * z + q)], 16)
-        v.transpose(T.xv[:, 2048 * z:2048 * z + 2048], T.xb[:, 2048 * z:2048 * z + 2048]).then_inc(S.xz, 1)
-
     def v_pf():
-        v.wait_ge(S.ln, 1)
         for n, k in enumerate(WINS):
             v.wait_ge(S["lst%d" % k], len(lengs[k]))
-            for t in range(4):
-                v.tensor_scalar(T.pf[:, 128 * n + t:128 * n + 128:4], T.lanes[:], T["li%d" % k][:, t:t + 1], None,
-                                ADD).then_inc(S.pf, 1)
+            for m in range(2):
+                v.tensor_scalar(T.pf[:, n, 0:2, 4 * m:4 * m + 4], T["li%d" % k][:], 32 * m, None, ADD).then_inc(S.pf0, 1)
+        if "pfd" not in CFG["a"] + CFG["v"]:
+            pf_double(v)
+
+    def pf_double(e):
+        for d in range(3):
+            e.wait_ge(S["pf%d" % d], 1 if d else 4)
+            c = 2 << d
+            move(e, T.pf[:, :, c:2 * c, :], T.pf[:, :, 0:c, :]).then_inc(S["pf%d" % (d + 1)], 1)
+
+    def piece_pf(eng, k):
+        eng.wait_ge(S.ln, 4)
+        eng.wait_ge(*((S.lsp, len(lengs["p"])) if k else (S.px, 1)))
+        slot = 4 + PIECES.index(0) if 0 in PIECES else 0
+        for e in range(4):
+            out = T.pfo[:, PIECES.index(k), :, 4 * e:4 * e + 4]
+            col = T.lp[:, e:e + 1] if k else T.px[:, slot, 2 * e + 1:2 * e + 2]
+            if eng is v:
+                v.tensor_scalar(out, T.lanes[:], col, None, ADD).then_inc(S["pfo%d" % k], 1)
+            else:
+                a.activation(out, T.lanes[:], ActivationFunctionType.Identity, bias=col).then_inc(S["pfo%d" % k], 1)
+
+    def t_offs():
+        for n, k in enumerate(PIECES):
+            te.wait_ge(S["pfo%d" % k], 4)
+            o = 1792 + 128 * n
+            te.transpose(T.ps_y[:, o:o + 128], T.pfo[:, n], T.ident[:]).then_inc(S.pt, 1)
+        te.wait_ge(S.pf3, 1)
+        for n in range(2):
+            o = 1536 + 128 * n
+            te.transpose(T.ps_y[:, o:o + 128], T.pf[:, n], T.ident[:]).then_inc(S.pt, 1)
 
     def v_offs():
-        v.wait_ge(S.pt, 2)
-        v.tensor_copy(T.offx[:], T.ps_p[:, 0:256]).then_inc(S.offx, 1)
+        n = 256 + (128 * len(PIECES) - 96 if PIECES else 0)
+        v.wait_ge(S.pt, 2 + len(PIECES))
+        v.tensor_copy(T.offx[:, 0:n], T.ps_y[:, 1536:1536 + n]).then_inc(S.offx, 1)
 
-    def gather_win(e, k, lo, hi):
-        if hi <= lo:
-            return
-        o = 128 * WINS.index(k)
+    def v_turn(z):
+        for q in range(4 // per):
+            v.wait_ge(S["xl%d" % (4 * z // per + q)], 16 * per)
+        v.transpose(T.xv[:, zc * z:zc * z + zc], T.xb[:, zc * z:zc * z + zc]).then_inc(S.xz, 1)
+
+    def gather_win(e, kh, lo, hi):
+        k, h = kh // 10, kh % 10
+        o = 128 * WINS.index(k) + (64 if kh in PE else 0)
         e.wait_ge(S.offx, 1)
-        e.wait_ge(S.xz, 4)
-        move(e, T["xg%d" % k][:, 16 * lo:16 * hi], T.xv[:].indirect(T.offx[:, o + lo:o + hi])).then_inc(S["gx%d" % k], 1)
+        e.wait_ge(S.xz, NZ)
+        move(e, T[("xf%d" if kh in PE else "xg%d") % k][:, 1024 * h + 16 * lo:1024 * h + 16 * hi],
+             T.xv[:, 64 * h:8192].indirect(T.offx[:, o + lo:o + hi])).then_inc(S["gx%d" % kh], 1)
 
-    def v_back(k):
-        v.wait_ge(S["gx%d" % k], int(CFG["cut"][k] > 0) + int(CFG["cut"][k] < 128))
-        for m in range(4):
+    def ngather(k, h):
+        return sum(1 for n in CFG["v"] + CFG["a"] if n.startswith("g%d%d:" % (k, h)))
+
+    freed = [None, None]
+
+    def t_unit(k, h):
+        te.wait_ge(S["gx%d%d" % (k, h)], ngather(k, h))
+        for m in range(2):
+            if freed[m]:
+                te.wait_ge(*freed[m])
+            freed[m] = (S["xe%d%d%d" % (k, h, m)], 1)
             for t in range(4):
-                v.transpose(T["ex%d" % k][:, :, 128 * m + t:128 * m + 128:4],
-                            T["xg%d" % k][:, 4 * m + t:2048:16]).then_inc(S["bk%d" % k], 1)
+                o = 1024 * h + 4 * m + t
+                te.transpose(T.ps_x[:, 512 * m + t:512 * m + 512:4], T["xf%d" % k][:, o:1024 * h + 1024:8],
+                             T.ident[:]).then_inc(S["xi%d%d%d" % (k, h, m)], 1)
+
+    def x_down(e, k, h, m):
+        e.wait_ge(S["xi%d%d%d" % (k, h, m)], 4)
+        o = 1024 * h + 512 * m
+        move(e, T["xt%d" % k][:, o:o + 512], T.ps_x[:, 512 * m:512 * m + 512]).then_inc(S["xe%d%d%d" % (k, h, m)], 1)
+
+    def v_back(k, h):
+        v.wait_ge(S["gx%d%d" % (k, h)], ngather(k, h))
+        for m in range(2):
+            for t in range(4):
+                o = 1024 * h + 4 * m + t
+                v.transpose(T["xs%d%d" % (k, h)][:, :, 128 * m + t:128 * m + 128:4],
+                            T["xg%d" % k][:, o:1024 * h + 1024:8]).then_inc(S["bk%d%d" % (k, h)], 1)
+
+    def s_ex(e, k, h, lo=0, hi=4):
+        e.wait_ge(S["bk%d%d" % (k, h)], 8)
+        for q in range(lo, hi):
+            o = 1024 * h + 256 * q
+            e.dma_start(T["xt%d" % k][:, o:o + 256], T["xs%d%d" % (k, h)][32 * q:32 * q + 32]).then_inc(S["ex%d%d" % (k, h)], 16)
+
+    def v_quant_unit(k, h):
+        if 10 * k + h in PE:
+            for m in range(2):
+                v.wait_ge(S["xe%d%d%d" % (k, h, m)], 1)
+        else:
+            v.wait_ge(S["ex%d%d" % (k, h)], 64)
+        c = slice(256 * h, 256 * h + 256)
+        v.quantize_mx(T["xq%d" % k][:, c], T["xp%d" % k][:, c],
+                      T["xt%d" % k][:, 1024 * h:1024 * h + 1024]).then_inc(S["qu%d%d" % (k, h)], 1)
 
     def copy(e, k, t):
         e.wait_ge(S["ga%d%d" % (k, t)], 16)
-        move(e, T["xt%d" % k][:, t:2048:4], T["xs%d" % k][:, 512 * t:512 * t + 512]).then_inc(S["xc%d" % k], 1)
+        move(e, T["xt%d" % k][:, :, t:512:4], T["xs%d" % k][:, 512 * t:512 * t + 512]).then_inc(S["xc%d" % k], 1)
+
+    def copy_part(e, k, lo, hi):
+        e.wait_ge(S["ga%d3" % k], 16)
+        move(e, T["xt%d" % k][:, lo:hi, 3:512:4], T["xs%d" % k][:, 1536 + 128 * lo:1536 + 128 * hi]).then_inc(S["xc%d" % k], 1)
+
+    def piece_gather(e, k):
+        n = PIECES.index(k)
+        e.wait_ge(S.offx, 1)
+        e.wait_ge(S.xz, NZ)
+        o = 256 + 128 * n
+        move(e, T.xo[:, 512 * n:512 * n + 512], T.xv[:].indirect(T.offx[:, o:o + 32])).then_inc(S["og%d" % k], 1)
+
+    def t_piece(k):
+        n = PIECES.index(k)
+        te.wait_ge(S["og%d" % k], 1)
+        b = 1 - n
+        if freed[b]:
+            te.wait_ge(*freed[b])
+        freed[b] = (S["oe%d" % k], 4)
+        for m in range(4):
+            o = 512 * b + 128 * m
+            te.transpose(T.ps_x[:, o:o + 128], T.xo[:, 512 * n + m:512 * n + 512:4], T.ident[:]).then_inc(S["ob%d" % k], 1)
+
+    def piece_down(e, k):
+        b = 1 - PIECES.index(k)
+        e.wait_ge(S["ob%d" % k], 4)
+        for m in range(4):
+            o = 512 * b + 128 * m
+            move(e, T["xt%d" % k][:, :, 128 * m + 3:128 * m + 128:4], T.ps_x[:, o:o + 128]).then_inc(S["oe%d" % k], 1)
 
     def v_quant(k):
-        if k in WINS:
-            v.wait_ge(S["ex%d" % k], 64)
-        else:
-            v.wait_ge(S["xc%d" % k], 4)
-        v.quantize_mx(T["xq%d" % k][:], T["xp%d" % k][:], T["xt%d" % k][:]).then_inc(S["qx%d" % k], 1)
-
-    def v_quant_half(h):
-        v.wait_ge(S["ex" + "ab"[h]], 32)
-        c = slice(256 * h, 256 * h + 256)
-        v.quantize_mx(T["xq%d" % last][:, c], T["xp%d" % last][:, c],
-                      T["xt%d" % last][:, 1024 * h:1024 * h + 1024]).then_inc(S["qh" + "ab"[h]], 1)
-
-    def v_wquant(k):
-        v.wait_ge(S["wd%d" % k], 1)
-        v.quantize_mx(T["wq%d" % k][:], T["wp%d" % k][:], T["wt%d" % k][:]).then_inc(S["qw%d" % k], 1)
-
-    def yhalf(e, h):
-        n = "ab"[h]
-        e.wait_ge(S["mm" + n], 1)
-        move(e, T.ys[:, ycols(last, 256 * h, 256 * h + 256)], T.ps_y[:, 1536 * h:1536 * h + 256]).then_inc(S["ev" + n], 1)
+        v.wait_ge(S["xc%d" % k], sum(1 for n in CFG["v"] + CFG["a"] if n.startswith(("c%d" % k, "cp%d" % k))))
+        if k in PIECES:
+            v.wait_ge(S["oe%d" % k], 4)
+        for q in range(4):
+            c = slice(128 * q, 128 * q + 128)
+            v.quantize_mx(T["xq%d" % k][:, c], T["xp%d" % k][:, c], T["xt%d" % k][:, q, :]).then_inc(S["qx%d" % k], 1)
 
     worder = [int(n[2]) for n in CFG["t"] if n.startswith("wb")]
     morder = [int(n[2]) for n in CFG["t"] if n.startswith("mm")]
 
-    def a_cv(b):
-        a.wait_ge(S["wl%d" % b], 16)
-        a.activation(T.wf[:, 512 * b:512 * b + 512], T.wb[:, 512 * b:512 * b + 512], COPY).then_inc(S["cv%d" % b], 1)
+    def w_cv(e, b):
+        e.wait_ge(S["wl%d" % b], 16)
+        move(e, T.wf[:, 512 * b:512 * b + 512], T.wb[:, 512 * b:512 * b + 512]).then_inc(S["cv%d" % b], 1)
+
+    def t_wf(b):
+        te.wait_ge(S["cv%d" % b], 1)
+        if b >= 2:
+            te.wait_ge(S["we%d" % (b - 2)], 1)
+        o = 512 * (b % 2)
+        for i in range(4):
+            c = 4 * b + i
+            te.transpose(T.ps_w[:, o + i:o + 512:4], T.wf[:, 128 * c:128 * c + 128], T.ident[:]).then_inc(S["wi%d" % b], 1)
 
     def a_we(b):
         a.wait_ge(S["wi%d" % b], 4)
-        o = 512 * (b % 3)
+        o = 512 * (b % 2)
         a.activation(T.wtr[:, 512 * b:512 * b + 512], T.ps_w[:, o:o + 512], COPY).then_inc(S["we%d" % b], 1)
 
     def w_gather(e, k):
         e.wait_ge(S.offw, 1)
-        for b in range(4):
-            e.wait_ge(S["we%d" % b], 1)
+        for b in range(1 if WEX else 4):
+            e.wait_ge(S["we%d" % b], 64 if WEX else 1)
         s = frm[k]
         move(e, T.wg[:, 512 * k:512 * k + 512], T.wtr[:].indirect(T.offw[:, 32 * s:32 * s + 32])).then_inc(S["wg%d" % k], 1)
 
     def wbank(k):
-        return 512 * ((worder.index(k) + 1) % 3)
+        return 512 * (worder.index(k) % 2)
+
+    def t_wb(k):
+        te.wait_ge(S["wg%d" % k], 1)
+        n = worder.index(k)
+        if n >= 2:
+            te.wait_ge(S["wd%d" % worder[n - 2]], 1)
+        o = wbank(k)
+        for t in range(4):
+            te.transpose(T.ps_w[:, o + t:o + 512:4], T.wg[:, 512 * k + t:512 * k + 512:4], T.ident[:]).then_inc(S["wv%d" % k], 1)
 
     def w_down(e, k):
         e.wait_ge(S["wv%d" % k], 4)
         move(e, T["wt%d" % k][:], T.ps_w[:, wbank(k):wbank(k) + 512]).then_inc(S["wd%d" % k], 1)
 
-    def ybank(k):
-        return 512 * morder.index(k)
-
-    def y_out(e, k):
-        e.wait_ge(S["mm%d" % k], 1)
-        move(e, T.ys[:, ycols(k)], T.ps_y[:, ybank(k):ybank(k) + 512]).then_inc(S["ev%d" % k], 1)
-
-    def a_yb():
-        yhalf(a, 1)
-        a.wait_ge(S.evb, 1)
-        a.dma_start(T.y[:, ycols(last, 256, 512)], T.ys[:, ycols(last, 256, 512)]).then_inc(S.stb, 16)
-        a.wait_ge(S.stb, 16)
-
-    def t_wf(b):
-        te.wait_ge(S["cv%d" % b], 1)
-        if b >= 3:
-            te.wait_ge(S["we%d" % (b - 3)], 1)
-        o = 512 * (b % 3)
-        for i in range(4):
-            c = 4 * b + i
-            te.transpose(T.ps_w[:, o + i:o + 512:4], T.wf[:, 128 * c:128 * c + 128], T.ident[:]).then_inc(S["wi%d" % b], 1)
-
-    def t_offs():
-        te.wait_ge(S.pf, 8)
-        for n in range(2):
-            te.transpose(T.ps_p[:, 128 * n:128 * n + 128], T.pf[:, 128 * n:128 * n + 128], T.ident[:]).then_inc(S.pt, 1)
-
-    def t_wb(k):
-        te.wait_ge(S["wg%d" % k], 1)
-        n = worder.index(k)
-        if n >= 3:
-            te.wait_ge(S["wd%d" % worder[n - 3]], 1)
-        o = wbank(k)
-        for t in range(4):
-            te.transpose(T.ps_w[:, o + t:o + 512:4], T.wg[:, 512 * k + t:512 * k + 512:4], T.ident[:]).then_inc(S["wv%d" % k], 1)
+    def v_wquant(k):
+        v.wait_ge(S["wd%d" % k], 1)
+        v.quantize_mx(T["wq%d" % k][:], T["wp%d" % k][:], T["wt%d" % k][:]).then_inc(S["qw%d" % k], 1)
 
     def t_mm(k):
         te.wait_ge(S["qw%d" % k], 1)
-        wq, wp = T["wq%d" % k][:], T["wp%d" % k][:]
         xq, xp = (T["rq%d" % k], T["rp%d" % k]) if k else (T.xq0, T.xp0)
-        if k != last:
-            if k:
-                te.wait_ge(S["arr%d" % k], narr)
-            else:
-                te.wait_ge(S.qx0, 1)
-            o = ybank(k)
-            te.matmul_mx(T.ps_y[:, o:o + 512], wq, wp, xq[:], xp[:], True, True).then_inc(S["mm%d" % k], 1)
-            return
-        te.wait_ge(S["ev%d" % morder[0]], 1)
-        for h in range(2):
-            c = slice(256 * h, 256 * h + 256)
-            te.wait_ge(S["ar" + "ab"[h]], narr)
-            te.matmul_mx(T.ps_y[:, 1536 * h:1536 * h + 256], wq, wp, xq[:, c], xp[:, c], True, True).then_inc(S["mm" + "ab"[h]], 1)
+        if k:
+            te.wait_ge(S["arr%d" % k], narr if "s%d" % k in CFG["g"] else 3 * narr // 4 if "sc%d" % k in CFG["g"] else 2 * narr)
+        else:
+            te.wait_ge(S.qx0, 4)
+        o = 512 * morder.index(k)
+        te.matmul_mx(T.ps_y[:, o:o + 512], T["wq%d" % k][:], T["wp%d" % k][:], xq[:], xp[:], True, True).then_inc(S["mm%d" % k], 1)
 
-    def listmove(k):
+    def mm_last(o, c):
+        return te.matmul_mx(T.ps_y[:, o:o + c.stop - c.start], T["wq%d" % LAST][:], T["wp%d" % LAST][:],
+                            T["rq%d" % LAST][:, c], T["rp%d" % LAST][:, c], True, True)
+
+    def nunit(k, h):
+        return 2 if 10 * k + h in PE else 1
+
+    def nev(k):
+        return nunit(k, 0) + nunit(k, 1) if k in WINS else 1
+
+    def unit_out(e, k, h, o, sem):
+        s = 4 * frm[k]
+        if 10 * k + h in PE:
+            for m in range(2):
+                move(e, T.ys[:, s:s + 4, 2 * h + m, :], T.ps_y[:, o + 128 * m:o + 128 * m + 128]).then_inc(sem, 1)
+        else:
+            move(e, T.ys[:, s:s + 4, 2 * h:2 * h + 2, :], T.ps_y[:, o:o + 256]).then_inc(sem, 1)
+
+    def t_mu():
+        te.wait_ge(S["qw%d" % LAST], 1)
+        te.wait_ge(S.offx, 1)
+        te.wait_ge(S.ar0, narr)
+        mm_last(1536, slice(0, 256)).then_inc(S.mu, 1)
+
+    def t_mh():
+        for h in range(2):
+            te.wait_ge(S["ev%d" % morder[h]], nev(morder[h]))
+        te.wait_ge(S.ar1, narr)
+        for h in range(2):
+            mm_last(512 * h, slice(256 + 128 * h, 384 + 128 * h)).then_inc(S["mh%d" % h], 1)
+
+    def y_out(e, k):
+        e.wait_ge(S["mm%d" % k], 1)
+        o, s = 512 * morder.index(k), 4 * frm[k]
+        if k in WINS:
+            for h in range(2):
+                unit_out(e, k, h, o + 256 * h, S["ev%d" % k])
+        else:
+            move(e, T.ys[:, s:s + 4], T.ps_y[:, o:o + 512]).then_inc(S["ev%d" % k], 1)
+
+    def y_unit(e):
+        e.wait_ge(S.mu, 1)
+        unit_out(e, LAST, 0, 1536, S.eu)
+
+    def y_half(e, h):
+        e.wait_ge(S["mh%d" % h], 1)
+        s = 4 * frm[LAST]
+        out = T.ys[:, s:s + 4, 2 + h, :] if nunit(LAST, 1) == 2 else T.ys[:, s + 2 * h:s + 2 * h + 2, 2:4, :]
+        move(e, out, T.ps_y[:, 512 * h:512 * h + 128]).then_inc(S["eh%d" % h], 1)
+        if h:
+            store_half(a, 1)
+
+    def store_runs(e, qs, h, sem):
+        for q in qs:
+            s = 4 * frm[LAST] + q
+            e.dma_start(T.y[:, 128 * s + 64 * h:128 * s + 64 * h + 64], T.ys[:, s, 2 * h:2 * h + 2, :]).then_inc(sem, 16)
+
+    def s_stu():
+        sy.wait_ge(S.eu, nunit(LAST, 0))
+        store_runs(sy, range(4), 0, S.stu)
+
+    def store_half(e, h):
+        if "stu" in CFG["s"]:
+            e.wait_ge(S["eh%d" % h], 1)
+            store_runs(e, (2 * h, 2 * h + 1), 1, S["sh%d" % h])
+            e.wait_ge(S["sh%d" % h], 32)
+            if e is sy:
+                sy.wait_ge(S.stu, 64)
+            return
+        e.wait_ge(S.eu, nunit(LAST, 0))
+        e.wait_ge(S["eh%d" % h], 1)
+        if nunit(LAST, 1) == 2:
+            e.wait_ge(S["eh%d" % (1 - h)], 1)
+        s = 4 * frm[LAST] + 2 * h
+        e.dma_start(T.y[:, 128 * s:128 * s + 256], T.ys[:, s:s + 2]).then_inc(S["sh%d" % h], 16)
+        e.wait_ge(S["sh%d" % h], 16)
+
+    def s_st(k):
+        sy.wait_ge(S["ev%d" % k], nev(k))
+        s = 4 * frm[k]
+        sy.dma_start(T.y[:, 128 * s:128 * s + 512], T.ys[:, s:s + 4]).then_inc(S["st%d" % k], 16)
+
+    def listmove(k, piece=False):
         s = frm[k]
         rid, pid = dst(s)
-        src = T.px if k in WINS else T.pk
-        return RemoteDMATransfer(dst_ids=[DstId(rid=rid, pnc=pid)], dma_engine_mask=bits(lengs[k]),
-                                 remote_sem=S["lst%d" % k], srcs=[src[:, 4 * s:4 * s + 4]], dsts=[T["li%d" % k][:]])
+        if piece:
+            src, land, sem = T.pxs[:], T.lp[:], S.lsp
+        elif k in WINS:
+            src, land, sem = T.pxu[:, WINS.index(k), :], T["li%d" % k][:], S["lst%d" % k]
+        else:
+            src, land, sem = T.pk[:, 4 * s:4 * s + nt[k]], T["li%d" % k][:, 0:nt[k]], S["lst%d" % k]
+        return RemoteDMATransfer(dst_ids=[DstId(rid=rid, pnc=pid)], dma_engine_mask=bits(lengs["p" if piece else k]),
+                                 remote_sem=sem, srcs=[src], dsts=[land])
 
     def g_l1():
         g.wait_ge(S.pk, 16)
         g.remote_dma_fused([listmove(1)], local_sem=S.ls1)
 
     def g_l23():
-        g.wait_ge(S.px, 1)
-        g.remote_dma_fused([listmove(2), listmove(3)], local_sem=S.lsent)
+        g.wait_ge(S.pxu, 2)
+        if 1 in PIECES:
+            g.wait_ge(S.pxs, 1)
+        g.remote_dma_fused([listmove(2), listmove(3)] + ([listmove(1, True)] if 1 in PIECES else []), local_sem=S.lsent)
 
     def gather(k, t):
+        g.wait_ge(*((S.lst1, len(lengs[1])) if k else (S.pk, 16)))
         idx = T["li%d" % k][:, t:t + 1] if k else T.pk[:, 4 * me + t:4 * me + t + 1]
         g.indirect_dma_start(T["xs%d" % k][:, 512 * t:512 * t + 512], None, T.x[:],
                              IndirectOffsetOnAxis(ap=idx, axis=0), bounds_check=ROWS - 1).then_inc(S["ga%d%d" % (k, t)], 16)
@@ -319,52 +567,61 @@ def rank_program(g, core, T, topo):
     def send(k, ready, arrived, c):
         e = topo.engines(core, cores[to[k]])
         rid, pid = dst(to[k])
-        g.wait_ge(ready, 1)
+        for r in ready:
+            g.wait_ge(*r)
         g.remote_dma(T["rq%d" % k][:, c].bitcast(dt.uint8), T["xq%d" % k][:, c].bitcast(dt.uint8),
                      arrived, S.csent, pid, rid, bits(e))
         g.remote_dma(T["rp%d" % k][:, c], T["xp%d" % k][:, c], arrived, S.csent, pid, rid, bits(e))
 
     def send_whole(k):
-        send(k, S["qx%d" % k], S["arr%d" % k], slice(0, XC))
+        ready = [(S["qu%d%d" % (k, h)], 1) for h in range(2)] if k in WINS else [(S["qx%d" % k], 4)]
+        send(k, ready, S["arr%d" % k], slice(0, XC))
 
-    def send_half(h):
-        send(last, S["qh" + "ab"[h]], S["ar" + "ab"[h]], slice(256 * h, 256 * h + 256))
+    def send_codes(k):
+        for r in [(S["qu%d%d" % (k, h)], 1) for h in range(2)] if k in WINS else [(S["qx%d" % k], 4)]:
+            g.wait_ge(*r)
+        rid, pid = dst(to[k])
+        g.remote_dma(T["rq%d" % k][:].bitcast(dt.uint8), T["xq%d" % k][:].bitcast(dt.uint8),
+                     S["arr%d" % k], S.csent, pid, rid, bits(off_chip))
 
-    def s_ex(k):
-        sy.wait_ge(S["bk%d" % k], 16)
-        for q in range(4):
-            sem = S["ex%d" % k] if k != last else S["ex" + "ab"[q // 2]]
-            sy.dma_start(T["xt%d" % k][:, 512 * q:512 * q + 512], T["ex%d" % k][32 * q:32 * q + 32]).then_inc(sem, 16)
+    def send_scales(*ks):
+        moves = []
+        for n, k in enumerate(ks):
+            rid, pid = dst(to[k])
+            moves.append(RemoteDMATransfer(dst_ids=[DstId(rid=rid, pnc=pid)], dma_engine_mask=bits(off_chip[4 * n:4 * n + 4]),
+                                           remote_sem=S["arr%d" % k], srcs=[T["xp%d" % k][:]], dsts=[T["rp%d" % k][:]]))
+        g.remote_dma_fused(moves, local_sem=S.csent)
 
-    def s_st(k):
-        sy.wait_ge(S["ev%d" % k], 1)
-        sy.dma_start(T.y[:, ycols(k)], T.ys[:, ycols(k)]).then_inc(S["st%d" % k], 16)
+    def send_half(k, h):
+        send(k, [(S["qu%d%d" % (k, h)], 1)], S["ar%d" % h] if k == LAST else S["arr%d" % k], slice(256 * h, 256 * h + 256))
 
-    def s_sta():
-        sy.wait_ge(S.eva, 1)
-        sy.dma_start(T.y[:, ycols(last, 0, 256)], T.ys[:, ycols(last, 0, 256)]).then_inc(S.sta, 16)
-
-    def play(order, plain, numbered):
+    def play(order, calls):
         for n in order:
-            if n in plain:
-                plain[n]()
-            else:
-                head = n.rstrip("0123456789")
-                numbered[head](*[int(c) for c in n[len(head):]])
+            head = n.rstrip("0123456789:")
+            rest = n[len(head):]
+            calls[head](*[int(c) for c in (rest.split(":") if ":" in rest else rest)])
 
-    play(CFG["v"], {"pos": v_pos, "woff": v_woff, "pf": v_pf, "offs": v_offs, "ya": lambda: yhalf(v, 0)},
-         {"turn": v_turn, "g": lambda k: gather_win(v, k, 0, CFG["cut"][k]), "back": v_back, "c": lambda k, t: copy(v, k, t),
-          "q": v_quant, "qh": v_quant_half, "wq": v_wquant, "y": lambda k: y_out(v, k), "wg": lambda k: w_gather(v, k),
-          "wd": lambda k: w_down(v, k)})
-    play(CFG["a"], {"yb": a_yb},
-         {"cv": a_cv, "we": a_we, "g": lambda k: gather_win(a, k, CFG["cut"][k], 128), "wg": lambda k: w_gather(a, k),
-          "wd": lambda k: w_down(a, k), "c": lambda k, t: copy(a, k, t), "y": lambda k: y_out(a, k)})
-    play(CFG["t"], {"offs": t_offs}, {"wf": t_wf, "wb": t_wb, "mm": t_mm})
-    play(CFG["g"], {"l1": g_l1, "l23": g_l23, "wl": lambda: g.wait_ge(S.lst1, len(lengs[1]))},
-         {"ga": gather, "s": send_whole, "sh": send_half})
-    play(CFG["s"], {"sta": s_sta}, {"ex": s_ex, "st": s_st})
+    def loads(e):
+        return {"pa": lambda q: load_pa(e, q), "lq": lambda q: load_lq(e, q), "w": lambda b: load_w(e, b),
+                "ex": lambda *r: s_ex(e, *r)}
+
+    def shared(e):
+        return {"g": lambda kh, lo, hi: gather_win(e, kh, lo, hi), "c": lambda k, t: copy(e, k, t), "y": lambda k: y_out(e, k),
+                "wg": lambda k: w_gather(e, k), "wd": lambda k: w_down(e, k), "cv": lambda b: w_cv(e, b),
+                "og": lambda k: piece_gather(e, k), "oe": lambda k: piece_down(e, k), "yu": lambda: y_unit(e), "wdup": lambda: w_dup(e), "pfd": lambda: pf_double(e),
+                "cp": lambda k, lo, hi: copy_part(e, k, lo, hi),
+                "yh": lambda h: y_half(e, h), "pfo": lambda k: piece_pf(e, k), "xe": lambda k, h, m: x_down(e, k, h, m)}
+
+    play(CFG["v"], dict(shared(v), wpos=v_wpos, wturn=v_wturn, pos=v_pos, woff=v_woff, pf=v_pf, offs=v_offs, turn=v_turn,
+                        back=v_back, q=v_quant, qu=v_quant_unit, wq=v_wquant))
+    play(CFG["a"], dict(shared(a), we=a_we, wex=a_wex, **loads(a)))
+    play(CFG["t"], {"offs": t_offs, "wf": t_wf, "wb": t_wb, "mm": t_mm, "ob": t_piece, "mu": t_mu, "mh": t_mh, "xb": t_unit})
+    play(CFG["g"], {"l": lambda *k: g_l1() if k == (1,) else g_l23(),
+                    "go": lambda: g.sem_inc(S.go, 1), "ga": gather, "s": send_whole, "sh": send_half,
+                    "sc": send_codes, "sp": send_scales})
+    play(CFG["s"], dict(loads(sy), sth=lambda: store_half(sy, 0), go=lambda: sy.wait_ge(S.go, 1), st=s_st, stu=s_stu, x=load_x))
     g.wait_ge(S.ls1, len(lengs[1]))
-    g.wait_ge(S.lsent, len(lengs[2]) + len(lengs[3]))
-    g.wait_ge(S.csent, 4 * narr)
-    for k in range(NR):
-        sy.wait_ge(S["st%d" % k] if k != last else S.sta, 16)
+    g.wait_ge(S.lsent, len(lengs[2]) + len(lengs[3]) + (len(lengs["p"]) if 1 in PIECES else 0))
+    g.wait_ge(S.csent, sum(narr // 2 if n[1] in "cp" else narr for n in CFG["g"] if n[0] == "s"))
+    for k in range(NR - 1):
+        sy.wait_ge(S["st%d" % k], 16)

from concourse.bass import DstId, RemoteDMATransfer, IndirectOffsetOnAxis
from concourse.mybir import dt, AluOpType, ActivationFunctionType

NR = 4
XC = 512
WC = 128
ROWS = 2048
WINS = (2, 3)
DMAS = (1, 0)
LAST = 3

CFG = {
    "depth": 7,
    "pieces": (),
    "pe": (21, 30),
    "nz": 4,
    "gfirst": False,
    "wide": True,
    "v": ["pos", "cv1", "wpos", "wdup", "turn0", "woff", "turn1", "pf", "turn2", "offs", "turn3", "g21:0:44", "g20:0:24",
          "c10", "back20", "c12", "c13", "q1", "g31:0:40", "back31", "qu21", "qu20", "wd2", "c01", "wd1", "wq1", "qu30",
          "wd0", "wq2", "qu31", "c00", "c03", "wq0", "q0", "y2", "wq3", "yu", "yh0"],
    "a": ["pa0", "pa1", "pa2", "pa3", "lq0", "lq1", "lq2", "lq3", "cv0", "cv2", "we0", "cv3", "we1", "we2", "we3", "wg2", "wg1",
          "g20:24:64", "g21:44:64", "c11", "g30:0:64", "xe210", "g31:40:64", "xe211", "wg0", "xe300", "xe301", "wg3",
          "c02", "y1", "wd3", "y0", "yh1"],
    "t": ["wf0", "wf1", "wf2", "wf3", "offs", "wb2", "wb1", "xb21", "xb30", "wb0", "mm1", "wb3", "mm2", "mm0", "mu", "mh"],
    "g": ["l1", "ga00", "l23", "ga10", "ga11", "ga12", "ga13", "ga01", "s1", "ga02", "s2", "ga03", "sh30", "sh31", "go"],
    "s": ["pa4", "w0", "w1", "w2", "w3", "x0:16", "ex20", "ex31", "go", "st1", "st2", "st0", "sth"],
}

SCRATCH = {
    "pk": ("sbuf", [128, 16], "int32"),
    "lq": ("sbuf", [128, 4, 16], "int32"),
    "pa": ("sbuf", [128, 6, 8], "int32"),
    "lu": ("sbuf", [128, 6, 8], "int32"),
    "lb": ("sbuf", [128, 6, 8], "int32"),
    "lc": ("sbuf", [128, 6, 8], "int32"),
    "lv": ("sbuf", [128, 6, 8], "int32"),
    "lw": ("sbuf", [128, 6, 8], "int32"),
    "px": ("sbuf", [128, 6, 8], "float32"),
    "pxu": ("sbuf", [128, 2, 8], "uint16"),
    "pxs": ("sbuf", [128, 4], "float32"),
    "lp": ("sbuf", [128, 4], "float32"),
    "wu": ("sbuf", [128, 4, 16], "int32"),
    "wx": ("sbuf", [128, 4, 16], "int32"),
    "wc": ("sbuf", [128, 4, 16], "int32"),
    "wy": ("sbuf", [128, 4, 16], "int32"),
    "wz": ("sbuf", [128, 4, 16], "int32"),
    "wpos": ("sbuf", [128, 4, 16], "float32"),
    "wn": ("sbuf", [128, 16, 128], "bfloat16"),
    "wv": ("sbuf", [128, 4, 512], "bfloat16"),
    "pw": ("sbuf", [128, 128], "float32"),
    "pwt": ("sbuf", [128, 128], "float32"),
    "offw": ("sbuf", [128, 128], "uint16"),
    "lanes": ("sbuf", [128, 32], "float32"),
    "pf": ("sbuf", [128, 2, 16, 8], "float32"),
    "pfo": ("sbuf", [128, 2, 8, 16], "float32"),
    "offx": ("sbuf", [128, 512], "uint16"),
    "ones": ("sbuf", [128, 128], "float32"),
    "cols": ("sbuf", [128, 128], "float32"),
    "parts": ("sbuf", [128, 128], "float32"),
    "ident": ("sbuf", [128, 128], "float32"),
    "wb": ("sbuf", [128, 2048], "bfloat16"),
    "wf": ("sbuf", [128, 2048], "float32"),
    "wtr": ("sbuf", [128, 2048], "bfloat16"),
    "wg": ("sbuf", [128, 2048], "float32"),
    "xb": ("sbuf", [128, 8192], "bfloat16"),
    "xv": ("sbuf", [128, 8192], "bfloat16"),
    "xo": ("sbuf", [128, 1024], "float32"),
    "ys": ("sbuf", [128, 16, 4, 32], "float32"),
    "ps_w": ("psum", [128, 1024], "float32"),
    "ps_x": ("psum", [128, 1024], "float32"),
    "ps_y": ("psum", [128, 2048], "float32"),
}
for _k in range(NR):
    if _k in WINS:
        SCRATCH["xg%d" % _k] = ("sbuf", [128, 2048], "bfloat16")
        SCRATCH["xf%d" % _k] = ("sbuf", [128, 2048], "float32")
        for _h in range(2):
            SCRATCH["xs%d%d" % (_k, _h)] = ("sbuf", [128, 4, 256], "bfloat16")
        SCRATCH["li%d" % _k] = ("sbuf", [128, 8], "uint16")
    else:
        SCRATCH["xs%d" % _k] = ("sbuf", [128, 2048], "bfloat16")
        if _k:
            SCRATCH["li%d" % _k] = ("sbuf", [128, 4], "int32")
    SCRATCH["xt%d" % _k] = ("sbuf", [128, 2048] if _k in WINS else [128, 4, 512], "bfloat16")
    if _k:
        SCRATCH["rq%d" % _k] = ("sbuf", [128, XC], "float8_e4m3fn_x4")
        SCRATCH["rp%d" % _k] = ("sbuf", [128, XC], "uint8")
    SCRATCH["xq%d" % _k] = ("sbuf", [128, XC], "float8_e4m3fn_x4")
    SCRATCH["xp%d" % _k] = ("sbuf", [128, XC], "uint8")
    SCRATCH["wt%d" % _k] = ("sbuf", [128, 512], "bfloat16")
    SCRATCH["wq%d" % _k] = ("sbuf", [128, WC], "float8_e4m3fn_x4")
    SCRATCH["wp%d" % _k] = ("sbuf", [128, WC], "uint8")

SEMAPHORES = ["id0", "id1", "id2", "id3", "go", "ln", "lq", "lq0", "pk", "pa", "la", "lv", "lw", "px", "pxu", "pw", "pwt",
              "offw", "pf0", "pf1", "pf2", "pf3", "wpos", "wa", "wy", "wz", "pt", "offx", "ls1", "lsent", "csent", "xz",
              "mu", "eu", "mh0", "mh1", "eh0", "eh1", "sh0", "sh1", "ar0", "ar1", "stu"]
SEMAPHORES += ["%s%d" % (n, k) for n in ("wl", "cv", "wi", "we", "wg", "wv", "wd", "qw", "mm", "ev", "st") for k in range(NR)]
SEMAPHORES += ["%s%d" % (n, k) for n in ("xc", "qx") for k in DMAS]
SEMAPHORES += ["%s%d" % (n, k) for n in ("og", "ob", "oe", "pfo") for k in CFG["pieces"]]
SEMAPHORES += ["pz", "lsp", "pxs"] if CFG["pieces"] else []
SEMAPHORES += ["%s%d%d" % (n, kh, m) for n in ("xi", "xe") for kh in CFG["pe"] for m in range(2)]
SEMAPHORES += ["%s%d%d" % (n, k, h) for n in ("gx", "bk", "ex", "qu") for k in WINS for h in range(2)]
SEMAPHORES += ["xl%d" % n for n in range(16)]
SEMAPHORES += ["%s%d" % (n, k) for n in ("lst", "arr") for k in range(1, NR)]
SEMAPHORES += ["ga%d%d" % (k, t) for k in DMAS for t in range(4)]

COPY = ActivationFunctionType.Copy
AND, SHR, ADD, MULT = AluOpType.bitwise_and, AluOpType.arith_shift_right, AluOpType.add, AluOpType.mult


def rank_program(g, core, T, topo):
    me = T.rank_of(core)
    if me is None:
        return
    S = T.sem
    cores = T.cores
    v, a, te, sy = g.vector, g.scalar, g.tensor, g.sync
    PIECES, PE, WEX = tuple(CFG["pieces"]), CFG["pe"], "wex" in CFG["a"]
    nt = {k: 3 if k in PIECES else 4 for k in DMAS}

    def direct(k):
        return sum(1 for r in range(NR)
                   if topo.same_plane(topo.chip(cores[r]), topo.chip(cores[(r + k) % NR])))
    steps = [0] + sorted(range(1, NR), key=direct)
    to = [(me + steps[k]) % NR for k in range(NR)]
    frm = [(me - steps[k]) % NR for k in range(NR)]

    def dst(r):
        rid, pid, _ = topo.addr(cores[r])
        return rid, pid

    def bits(engs):
        return sum(1 << e for e in engs)

    off_chip = topo.engines(core, cores[frm[1]])
    lengs = {1: off_chip[0:4], 2: off_chip[4:6], 3: off_chip[6:8], "p": off_chip[0:2]}
    if CFG.get("wide"):
        lengs = {1: off_chip[0:4], 2: off_chip[0:4], 3: off_chip[4:8]}
    narr = 2 * len(off_chip)

    def move(e, out, src):
        return v.tensor_copy(out, src) if e is v else a.activation(out, src, COPY)

    sy.dma_start(T.pk[:], T.pick[:]).then_inc(S.pk, 16)
    def load_pa(e, q):
        if q < 4:
            e.dma_start(T.pa[16 * q:16 * q + 16, 0:4, :], T.pick[q:128:4, :]).then_inc(S.pa, 16)
        else:
            e.dma_start(T.pa[64:128, 0:4, :], T.pick[:]).then_inc(S.pa, 16)

    for n, k in enumerate(PIECES):
        sy.dma_start(T.pa[0:32, 4 + n, :], T.pick[:, 4 * frm[k] + 2:4 * frm[k] + 4]).then_inc(S.pa, 16)
    nq = 1 if CFG["gfirst"] is True else 0

    def load_lq(e, q):
        e.dma_start(T.lq[32 * q:32 * q + 32], T.pick[:]).then_inc(S.lq0 if e is g else S.lq, 16)

    if nq:
        load_lq(g, 0)

    def load_w(e, b):
        e.dma_start(T.wb[:, 512 * b:512 * b + 512], T.w[512 * b:512 * b + 512, :]).then_inc(S["wl%d" % b], 16)

    if CFG["gfirst"] == "w":
        load_w(g, 3)

    NZ = CFG["nz"]
    per = 4 * NZ // 16
    zr, zc = ROWS // NZ, 8192 // NZ

    def load_x(lo, hi):
        for n in range(lo, hi):
            z, q = n // 4, n % 4
            if n % per == 0 and n // per >= CFG["depth"]:
                sy.wait_ge(S["xl%d" % (n // per - CFG["depth"])], 16 * per)
            sy.dma_start(T.xb[32 * q:32 * q + 32, zc * z:zc * z + zc],
                         T.x[zr * z:zr * z + zr, 128 * q:128 * q + 128]).then_inc(S["xl%d" % (n // per)], 16)

    v.memset(T.ones[:], 1.0).then_inc(S.id0, 1)
    v.wait_ge(S.id0, 1)
    v.tensor_tensor_scan(T.cols[:], T.ones[:], T.ones[:], 0.0, MULT, ADD).then_inc(S.id1, 1)
    for m in range(4 if PIECES else 0):
        v.memset(T.lanes[:, m:32:4], 32.0 * m).then_inc(S.ln, 1)
    v.wait_ge(S.id1, 1)
    v.transpose(T.parts[:], T.cols[:]).then_inc(S.id2, 1)
    if PIECES:
        for part in (slice(32, 64), slice(64, 128)):
            v.memset(T.pa[part, 4:6, :], 0).then_inc(S.pz, 1)
    v.wait_ge(S.id2, 1)
    for q in range(4):
        part = slice(32 * q, 32 * q + 32)
        v.tensor_scalar(T.ident[part, :], T.cols[part, :], T.parts[part, 32 * q:32 * q + 1], None,
                        AluOpType.is_equal).then_inc(S.id3, 1)
    te.wait_ge(S.id3, 4)

    def v_pos():
        v.wait_ge(S.pa, 16 * (5 + len(PIECES)))
        n = 4 + len(PIECES)
        if PIECES:
            v.wait_ge(S.pz, 2)
        nb = zr // 32
        v.tensor_scalar(T.lu[:, 0:n], T.pa[:, 0:n], 5, 64 - nb, SHR, AND).then_inc(S.la, 1)
        v.tensor_scalar(T.lb[:, 0:n], T.pa[:, 0:n], nb - 1, None, AND).then_inc(S.la, 1)
        v.tensor_scalar(T.lc[:, 0:n], T.pa[:, 0:n], nb.bit_length() - 1, 31, SHR, AND).then_inc(S.la, 1)
        v.wait_ge(S.la, 3)
        v.tensor_tensor(T.lv[:, 0:n], T.lu[:, 0:n], T.lb[:, 0:n], ADD).then_inc(S.lv, 1)
        v.wait_ge(S.lv, 1)
        v.tensor_scalar(T.lw[:, 0:n], T.lv[:, 0:n], 128, None, MULT).then_inc(S.lw, 1)
        v.wait_ge(S.lw, 1)
        v.tensor_tensor(T.px[:, 0:n], T.lw[:, 0:n], T.lc[:, 0:n], ADD).then_inc(S.px, 1)
        v.wait_ge(S.px, 1)
        for n, k in enumerate(WINS):
            s = frm[k]
            v.tensor_copy(T.pxu[:, n, :], T.px[:, s // 2:4:2, 4 * (s % 2):4 * (s % 2) + 4]).then_inc(S.pxu, 1)
        if 1 in PIECES:
            v.tensor_copy(T.pxs[:], T.px[:, 4 + PIECES.index(1), 1:8:2]).then_inc(S.pxs, 1)

    def v_wpos():
        v.wait_ge(S.lq, 16 * (4 - nq))
        if nq:
            v.wait_ge(S.lq0, 16)
        if not WEX:
            v.tensor_copy(T.wpos[:], T.lq[:]).then_inc(S.wpos, 1)
            return
        v.tensor_scalar(T.wu[:], T.lq[:], 5, 48, SHR, AND).then_inc(S.wa, 1)
        v.tensor_scalar(T.wx[:], T.lq[:], 15, None, AND).then_inc(S.wa, 1)
        v.tensor_scalar(T.wc[:], T.lq[:], 4, 31, SHR, AND).then_inc(S.wa, 1)
        v.wait_ge(S.wa, 3)
        v.tensor_tensor(T.wy[:], T.wu[:], T.wx[:], ADD).then_inc(S.wy, 1)
        v.wait_ge(S.wy, 1)
        v.tensor_scalar(T.wz[:], T.wy[:], 32, None, MULT).then_inc(S.wz, 1)
        v.wait_ge(S.wz, 1)
        v.tensor_tensor(T.wpos[:], T.wz[:], T.wc[:], ADD).then_inc(S.wpos, 1)

    def w_dup(e):
        e.wait_ge(S.wpos, 1)
        for s in range(NR):
            for d in range(2):
                o = 32 * s + 16 * d
                move(e, T.pw[:, o:o + 16], T.wpos[:, :, 4 * s:4 * s + 4]).then_inc(S.pw, 1)

    def v_wturn():
        v.wait_ge(S.wl0, 16)
        for m in range(4):
            v.transpose(T.wv[:, m, :], T.wn[:, :, m:128:4]).then_inc(S.wi0, 1)

    def a_wex():
        a.wait_ge(S.wi0, 4)
        for q in range(4):
            a.dma_start(T.wtr[:, 512 * q:512 * q + 512], T.wv[32 * q:32 * q + 32]).then_inc(S.we0, 16)

    def v_woff():
        v.wait_ge(S.pw, 8)
        v.transpose(T.pwt[:], T.pw[:]).then_inc(S.pwt, 1)
        v.wait_ge(S.pwt, 1)
        v.tensor_copy(T.offw[:], T.pwt[:]).then_inc(S.offw, 1)

    def v_pf():
        for n, k in enumerate(WINS):
            v.wait_ge(S["lst%d" % k], len(lengs[k]))
            for m in range(2):
                v.tensor_scalar(T.pf[:, n, 0:2, 4 * m:4 * m + 4], T["li%d" % k][:], 32 * m, None, ADD).then_inc(S.pf0, 1)
        if "pfd" not in CFG["a"] + CFG["v"]:
            pf_double(v)

    def pf_double(e):
        for d in range(3):
            e.wait_ge(S["pf%d" % d], 1 if d else 4)
            c = 2 << d
            move(e, T.pf[:, :, c:2 * c, :], T.pf[:, :, 0:c, :]).then_inc(S["pf%d" % (d + 1)], 1)

    def piece_pf(eng, k):
        eng.wait_ge(S.ln, 4)
        eng.wait_ge(*((S.lsp, len(lengs["p"])) if k else (S.px, 1)))
        slot = 4 + PIECES.index(0) if 0 in PIECES else 0
        for e in range(4):
            out = T.pfo[:, PIECES.index(k), :, 4 * e:4 * e + 4]
            col = T.lp[:, e:e + 1] if k else T.px[:, slot, 2 * e + 1:2 * e + 2]
            if eng is v:
                v.tensor_scalar(out, T.lanes[:], col, None, ADD).then_inc(S["pfo%d" % k], 1)
            else:
                a.activation(out, T.lanes[:], ActivationFunctionType.Identity, bias=col).then_inc(S["pfo%d" % k], 1)

    def t_offs():
        for n, k in enumerate(PIECES):
            te.wait_ge(S["pfo%d" % k], 4)
            o = 1792 + 128 * n
            te.transpose(T.ps_y[:, o:o + 128], T.pfo[:, n], T.ident[:]).then_inc(S.pt, 1)
        te.wait_ge(S.pf3, 1)
        for n in range(2):
            o = 1536 + 128 * n
            te.transpose(T.ps_y[:, o:o + 128], T.pf[:, n], T.ident[:]).then_inc(S.pt, 1)

    def v_offs():
        n = 256 + (128 * len(PIECES) - 96 if PIECES else 0)
        v.wait_ge(S.pt, 2 + len(PIECES))
        v.tensor_copy(T.offx[:, 0:n], T.ps_y[:, 1536:1536 + n]).then_inc(S.offx, 1)

    def v_turn(z):
        for q in range(4 // per):
            v.wait_ge(S["xl%d" % (4 * z // per + q)], 16 * per)
        v.transpose(T.xv[:, zc * z:zc * z + zc], T.xb[:, zc * z:zc * z + zc]).then_inc(S.xz, 1)

    def gather_win(e, kh, lo, hi):
        k, h = kh // 10, kh % 10
        o = 128 * WINS.index(k) + (64 if kh in PE else 0)
        e.wait_ge(S.offx, 1)
        e.wait_ge(S.xz, NZ)
        move(e, T[("xf%d" if kh in PE else "xg%d") % k][:, 1024 * h + 16 * lo:1024 * h + 16 * hi],
             T.xv[:, 64 * h:8192].indirect(T.offx[:, o + lo:o + hi])).then_inc(S["gx%d" % kh], 1)

    def ngather(k, h):
        return sum(1 for n in CFG["v"] + CFG["a"] if n.startswith("g%d%d:" % (k, h)))

    freed = [None, None]

    def t_unit(k, h):
        te.wait_ge(S["gx%d%d" % (k, h)], ngather(k, h))
        for m in range(2):
            if freed[m]:
                te.wait_ge(*freed[m])
            freed[m] = (S["xe%d%d%d" % (k, h, m)], 1)
            for t in range(4):
                o = 1024 * h + 4 * m + t
                te.transpose(T.ps_x[:, 512 * m + t:512 * m + 512:4], T["xf%d" % k][:, o:1024 * h + 1024:8],
                             T.ident[:]).then_inc(S["xi%d%d%d" % (k, h, m)], 1)

    def x_down(e, k, h, m):
        e.wait_ge(S["xi%d%d%d" % (k, h, m)], 4)
        o = 1024 * h + 512 * m
        move(e, T["xt%d" % k][:, o:o + 512], T.ps_x[:, 512 * m:512 * m + 512]).then_inc(S["xe%d%d%d" % (k, h, m)], 1)

    def v_back(k, h):
        v.wait_ge(S["gx%d%d" % (k, h)], ngather(k, h))
        for m in range(2):
            for t in range(4):
                o = 1024 * h + 4 * m + t
                v.transpose(T["xs%d%d" % (k, h)][:, :, 128 * m + t:128 * m + 128:4],
                            T["xg%d" % k][:, o:1024 * h + 1024:8]).then_inc(S["bk%d%d" % (k, h)], 1)

    def s_ex(e, k, h, lo=0, hi=4):
        e.wait_ge(S["bk%d%d" % (k, h)], 8)
        for q in range(lo, hi):
            o = 1024 * h + 256 * q
            e.dma_start(T["xt%d" % k][:, o:o + 256], T["xs%d%d" % (k, h)][32 * q:32 * q + 32]).then_inc(S["ex%d%d" % (k, h)], 16)

    def v_quant_unit(k, h):
        if 10 * k + h in PE:
            for m in range(2):
                v.wait_ge(S["xe%d%d%d" % (k, h, m)], 1)
        else:
            v.wait_ge(S["ex%d%d" % (k, h)], 64)
        c = slice(256 * h, 256 * h + 256)
        v.quantize_mx(T["xq%d" % k][:, c], T["xp%d" % k][:, c],
                      T["xt%d" % k][:, 1024 * h:1024 * h + 1024]).then_inc(S["qu%d%d" % (k, h)], 1)

    def copy(e, k, t):
        e.wait_ge(S["ga%d%d" % (k, t)], 16)
        move(e, T["xt%d" % k][:, :, t:512:4], T["xs%d" % k][:, 512 * t:512 * t + 512]).then_inc(S["xc%d" % k], 1)

    def copy_part(e, k, lo, hi):
        e.wait_ge(S["ga%d3" % k], 16)
        move(e, T["xt%d" % k][:, lo:hi, 3:512:4], T["xs%d" % k][:, 1536 + 128 * lo:1536 + 128 * hi]).then_inc(S["xc%d" % k], 1)

    def piece_gather(e, k):
        n = PIECES.index(k)
        e.wait_ge(S.offx, 1)
        e.wait_ge(S.xz, NZ)
        o = 256 + 128 * n
        move(e, T.xo[:, 512 * n:512 * n + 512], T.xv[:].indirect(T.offx[:, o:o + 32])).then_inc(S["og%d" % k], 1)

    def t_piece(k):
        n = PIECES.index(k)
        te.wait_ge(S["og%d" % k], 1)
        b = 1 - n
        if freed[b]:
            te.wait_ge(*freed[b])
        freed[b] = (S["oe%d" % k], 4)
        for m in range(4):
            o = 512 * b + 128 * m
            te.transpose(T.ps_x[:, o:o + 128], T.xo[:, 512 * n + m:512 * n + 512:4], T.ident[:]).then_inc(S["ob%d" % k], 1)

    def piece_down(e, k):
        b = 1 - PIECES.index(k)
        e.wait_ge(S["ob%d" % k], 4)
        for m in range(4):
            o = 512 * b + 128 * m
            move(e, T["xt%d" % k][:, :, 128 * m + 3:128 * m + 128:4], T.ps_x[:, o:o + 128]).then_inc(S["oe%d" % k], 1)

    def v_quant(k):
        v.wait_ge(S["xc%d" % k], sum(1 for n in CFG["v"] + CFG["a"] if n.startswith(("c%d" % k, "cp%d" % k))))
        if k in PIECES:
            v.wait_ge(S["oe%d" % k], 4)
        for q in range(4):
            c = slice(128 * q, 128 * q + 128)
            v.quantize_mx(T["xq%d" % k][:, c], T["xp%d" % k][:, c], T["xt%d" % k][:, q, :]).then_inc(S["qx%d" % k], 1)

    worder = [int(n[2]) for n in CFG["t"] if n.startswith("wb")]
    morder = [int(n[2]) for n in CFG["t"] if n.startswith("mm")]

    def w_cv(e, b):
        e.wait_ge(S["wl%d" % b], 16)
        move(e, T.wf[:, 512 * b:512 * b + 512], T.wb[:, 512 * b:512 * b + 512]).then_inc(S["cv%d" % b], 1)

    def t_wf(b):
        te.wait_ge(S["cv%d" % b], 1)
        if b >= 2:
            te.wait_ge(S["we%d" % (b - 2)], 1)
        o = 512 * (b % 2)
        for i in range(4):
            c = 4 * b + i
            te.transpose(T.ps_w[:, o + i:o + 512:4], T.wf[:, 128 * c:128 * c + 128], T.ident[:]).then_inc(S["wi%d" % b], 1)

    def a_we(b):
        a.wait_ge(S["wi%d" % b], 4)
        o = 512 * (b % 2)
        a.activation(T.wtr[:, 512 * b:512 * b + 512], T.ps_w[:, o:o + 512], COPY).then_inc(S["we%d" % b], 1)

    def w_gather(e, k):
        e.wait_ge(S.offw, 1)
        for b in range(1 if WEX else 4):
            e.wait_ge(S["we%d" % b], 64 if WEX else 1)
        s = frm[k]
        move(e, T.wg[:, 512 * k:512 * k + 512], T.wtr[:].indirect(T.offw[:, 32 * s:32 * s + 32])).then_inc(S["wg%d" % k], 1)

    def wbank(k):
        return 512 * (worder.index(k) % 2)

    def t_wb(k):
        te.wait_ge(S["wg%d" % k], 1)
        n = worder.index(k)
        if n >= 2:
            te.wait_ge(S["wd%d" % worder[n - 2]], 1)
        o = wbank(k)
        for t in range(4):
            te.transpose(T.ps_w[:, o + t:o + 512:4], T.wg[:, 512 * k + t:512 * k + 512:4], T.ident[:]).then_inc(S["wv%d" % k], 1)

    def w_down(e, k):
        e.wait_ge(S["wv%d" % k], 4)
        move(e, T["wt%d" % k][:], T.ps_w[:, wbank(k):wbank(k) + 512]).then_inc(S["wd%d" % k], 1)

    def v_wquant(k):
        v.wait_ge(S["wd%d" % k], 1)
        v.quantize_mx(T["wq%d" % k][:], T["wp%d" % k][:], T["wt%d" % k][:]).then_inc(S["qw%d" % k], 1)

    def t_mm(k):
        te.wait_ge(S["qw%d" % k], 1)
        xq, xp = (T["rq%d" % k], T["rp%d" % k]) if k else (T.xq0, T.xp0)
        if k:
            te.wait_ge(S["arr%d" % k], narr if "s%d" % k in CFG["g"] else 3 * narr // 4 if "sc%d" % k in CFG["g"] else 2 * narr)
        else:
            te.wait_ge(S.qx0, 4)
        o = 512 * morder.index(k)
        te.matmul_mx(T.ps_y[:, o:o + 512], T["wq%d" % k][:], T["wp%d" % k][:], xq[:], xp[:], True, True).then_inc(S["mm%d" % k], 1)

    def mm_last(o, c):
        return te.matmul_mx(T.ps_y[:, o:o + c.stop - c.start], T["wq%d" % LAST][:], T["wp%d" % LAST][:],
                            T["rq%d" % LAST][:, c], T["rp%d" % LAST][:, c], True, True)

    def nunit(k, h):
        return 2 if 10 * k + h in PE else 1

    def nev(k):
        return nunit(k, 0) + nunit(k, 1) if k in WINS else 1

    def unit_out(e, k, h, o, sem):
        s = 4 * frm[k]
        if 10 * k + h in PE:
            for m in range(2):
                move(e, T.ys[:, s:s + 4, 2 * h + m, :], T.ps_y[:, o + 128 * m:o + 128 * m + 128]).then_inc(sem, 1)
        else:
            move(e, T.ys[:, s:s + 4, 2 * h:2 * h + 2, :], T.ps_y[:, o:o + 256]).then_inc(sem, 1)

    def t_mu():
        te.wait_ge(S["qw%d" % LAST], 1)
        te.wait_ge(S.offx, 1)
        te.wait_ge(S.ar0, narr)
        mm_last(1536, slice(0, 256)).then_inc(S.mu, 1)

    def t_mh():
        for h in range(2):
            te.wait_ge(S["ev%d" % morder[h]], nev(morder[h]))
        te.wait_ge(S.ar1, narr)
        for h in range(2):
            mm_last(512 * h, slice(256 + 128 * h, 384 + 128 * h)).then_inc(S["mh%d" % h], 1)

    def y_out(e, k):
        e.wait_ge(S["mm%d" % k], 1)
        o, s = 512 * morder.index(k), 4 * frm[k]
        if k in WINS:
            for h in range(2):
                unit_out(e, k, h, o + 256 * h, S["ev%d" % k])
        else:
            move(e, T.ys[:, s:s + 4], T.ps_y[:, o:o + 512]).then_inc(S["ev%d" % k], 1)

    def y_unit(e):
        e.wait_ge(S.mu, 1)
        unit_out(e, LAST, 0, 1536, S.eu)

    def y_half(e, h):
        e.wait_ge(S["mh%d" % h], 1)
        s = 4 * frm[LAST]
        out = T.ys[:, s:s + 4, 2 + h, :] if nunit(LAST, 1) == 2 else T.ys[:, s + 2 * h:s + 2 * h + 2, 2:4, :]
        move(e, out, T.ps_y[:, 512 * h:512 * h + 128]).then_inc(S["eh%d" % h], 1)
        if h:
            store_half(a, 1)

    def store_runs(e, qs, h, sem):
        for q in qs:
            s = 4 * frm[LAST] + q
            e.dma_start(T.y[:, 128 * s + 64 * h:128 * s + 64 * h + 64], T.ys[:, s, 2 * h:2 * h + 2, :]).then_inc(sem, 16)

    def s_stu():
        sy.wait_ge(S.eu, nunit(LAST, 0))
        store_runs(sy, range(4), 0, S.stu)

    def store_half(e, h):
        if "stu" in CFG["s"]:
            e.wait_ge(S["eh%d" % h], 1)
            store_runs(e, (2 * h, 2 * h + 1), 1, S["sh%d" % h])
            e.wait_ge(S["sh%d" % h], 32)
            if e is sy:
                sy.wait_ge(S.stu, 64)
            return
        e.wait_ge(S.eu, nunit(LAST, 0))
        e.wait_ge(S["eh%d" % h], 1)
        if nunit(LAST, 1) == 2:
            e.wait_ge(S["eh%d" % (1 - h)], 1)
        s = 4 * frm[LAST] + 2 * h
        e.dma_start(T.y[:, 128 * s:128 * s + 256], T.ys[:, s:s + 2]).then_inc(S["sh%d" % h], 16)
        e.wait_ge(S["sh%d" % h], 16)

    def s_st(k):
        sy.wait_ge(S["ev%d" % k], nev(k))
        s = 4 * frm[k]
        sy.dma_start(T.y[:, 128 * s:128 * s + 512], T.ys[:, s:s + 4]).then_inc(S["st%d" % k], 16)

    def listmove(k, piece=False):
        s = frm[k]
        rid, pid = dst(s)
        if piece:
            src, land, sem = T.pxs[:], T.lp[:], S.lsp
        elif k in WINS:
            src, land, sem = T.pxu[:, WINS.index(k), :], T["li%d" % k][:], S["lst%d" % k]
        else:
            src, land, sem = T.pk[:, 4 * s:4 * s + nt[k]], T["li%d" % k][:, 0:nt[k]], S["lst%d" % k]
        return RemoteDMATransfer(dst_ids=[DstId(rid=rid, pnc=pid)], dma_engine_mask=bits(lengs["p" if piece else k]),
                                 remote_sem=sem, srcs=[src], dsts=[land])

    def g_l1():
        g.wait_ge(S.pk, 16)
        g.remote_dma_fused([listmove(1)], local_sem=S.ls1)

    def g_l23():
        g.wait_ge(S.pxu, 2)
        if 1 in PIECES:
            g.wait_ge(S.pxs, 1)
        g.remote_dma_fused([listmove(2), listmove(3)] + ([listmove(1, True)] if 1 in PIECES else []), local_sem=S.lsent)

    def gather(k, t):
        g.wait_ge(*((S.lst1, len(lengs[1])) if k else (S.pk, 16)))
        idx = T["li%d" % k][:, t:t + 1] if k else T.pk[:, 4 * me + t:4 * me + t + 1]
        g.indirect_dma_start(T["xs%d" % k][:, 512 * t:512 * t + 512], None, T.x[:],
                             IndirectOffsetOnAxis(ap=idx, axis=0), bounds_check=ROWS - 1).then_inc(S["ga%d%d" % (k, t)], 16)

    def send(k, ready, arrived, c):
        e = topo.engines(core, cores[to[k]])
        rid, pid = dst(to[k])
        for r in ready:
            g.wait_ge(*r)
        g.remote_dma(T["rq%d" % k][:, c].bitcast(dt.uint8), T["xq%d" % k][:, c].bitcast(dt.uint8),
                     arrived, S.csent, pid, rid, bits(e))
        g.remote_dma(T["rp%d" % k][:, c], T["xp%d" % k][:, c], arrived, S.csent, pid, rid, bits(e))

    def send_whole(k):
        ready = [(S["qu%d%d" % (k, h)], 1) for h in range(2)] if k in WINS else [(S["qx%d" % k], 4)]
        send(k, ready, S["arr%d" % k], slice(0, XC))

    def send_codes(k):
        for r in [(S["qu%d%d" % (k, h)], 1) for h in range(2)] if k in WINS else [(S["qx%d" % k], 4)]:
            g.wait_ge(*r)
        rid, pid = dst(to[k])
        g.remote_dma(T["rq%d" % k][:].bitcast(dt.uint8), T["xq%d" % k][:].bitcast(dt.uint8),
                     S["arr%d" % k], S.csent, pid, rid, bits(off_chip))

    def send_scales(*ks):
        moves = []
        for n, k in enumerate(ks):
            rid, pid = dst(to[k])
            moves.append(RemoteDMATransfer(dst_ids=[DstId(rid=rid, pnc=pid)], dma_engine_mask=bits(off_chip[4 * n:4 * n + 4]),
                                           remote_sem=S["arr%d" % k], srcs=[T["xp%d" % k][:]], dsts=[T["rp%d" % k][:]]))
        g.remote_dma_fused(moves, local_sem=S.csent)

    def send_half(k, h):
        send(k, [(S["qu%d%d" % (k, h)], 1)], S["ar%d" % h] if k == LAST else S["arr%d" % k], slice(256 * h, 256 * h + 256))

    def play(order, calls):
        for n in order:
            head = n.rstrip("0123456789:")
            rest = n[len(head):]
            calls[head](*[int(c) for c in (rest.split(":") if ":" in rest else rest)])

    def loads(e):
        return {"pa": lambda q: load_pa(e, q), "lq": lambda q: load_lq(e, q), "w": lambda b: load_w(e, b),
                "ex": lambda *r: s_ex(e, *r)}

    def shared(e):
        return {"g": lambda kh, lo, hi: gather_win(e, kh, lo, hi), "c": lambda k, t: copy(e, k, t), "y": lambda k: y_out(e, k),
                "wg": lambda k: w_gather(e, k), "wd": lambda k: w_down(e, k), "cv": lambda b: w_cv(e, b),
                "og": lambda k: piece_gather(e, k), "oe": lambda k: piece_down(e, k), "yu": lambda: y_unit(e), "wdup": lambda: w_dup(e), "pfd": lambda: pf_double(e),
                "cp": lambda k, lo, hi: copy_part(e, k, lo, hi),
                "yh": lambda h: y_half(e, h), "pfo": lambda k: piece_pf(e, k), "xe": lambda k, h, m: x_down(e, k, h, m)}

    play(CFG["v"], dict(shared(v), wpos=v_wpos, wturn=v_wturn, pos=v_pos, woff=v_woff, pf=v_pf, offs=v_offs, turn=v_turn,
                        back=v_back, q=v_quant, qu=v_quant_unit, wq=v_wquant))
    play(CFG["a"], dict(shared(a), we=a_we, wex=a_wex, **loads(a)))
    play(CFG["t"], {"offs": t_offs, "wf": t_wf, "wb": t_wb, "mm": t_mm, "ob": t_piece, "mu": t_mu, "mh": t_mh, "xb": t_unit})
    play(CFG["g"], {"l": lambda *k: g_l1() if k == (1,) else g_l23(),
                    "go": lambda: g.sem_inc(S.go, 1), "ga": gather, "s": send_whole, "sh": send_half,
                    "sc": send_codes, "sp": send_scales})
    play(CFG["s"], dict(loads(sy), sth=lambda: store_half(sy, 0), go=lambda: sy.wait_ge(S.go, 1), st=s_st, stu=s_stu, x=load_x))
    g.wait_ge(S.ls1, len(lengs[1]))
    g.wait_ge(S.lsent, len(lengs[2]) + len(lengs[3]) + (len(lengs["p"]) if 1 in PIECES else 0))
    g.wait_ge(S.csent, sum(narr // 2 if n[1] in "cp" else narr for n in CFG["g"] if n[0] == "s"))
    for k in range(NR - 1):
        sy.wait_ge(S["st%d" % k], 16)
